import numpy as np
import ml_dtypes


def mxq(x, axis, fmt="e4m3"):
    dtype, down = {"e4m3": (ml_dtypes.float8_e4m3fn, 7), "e5m2": (ml_dtypes.float8_e5m2, 14)}[fmt]
    v = np.moveaxis(np.asarray(x, np.float32).astype(ml_dtypes.bfloat16).astype(np.float64), axis, -1)
    blocks = v.reshape(v.shape[:-1] + (-1, 32))
    amax = np.abs(blocks).max(-1, keepdims=True)
    byte = np.maximum(np.where(amax > 0, np.frexp(amax)[1] - 1 + 127, 0) - down, 1)
    scale = np.exp2(byte - 127.0)
    codes = (blocks / scale).astype(np.float32).astype(dtype).astype(np.float64)
    return np.moveaxis((codes * scale).reshape(v.shape), -1, axis)


WIDE = False


def mx_kscale(k):
    if not WIDE:
        return np.ones(k)
    levels = np.array([10, -10, 5, -5, 0])
    if k % 512:
        return np.exp2(np.random.permutation(np.resize(levels, k // 32))).repeat(32)
    a = np.empty((k // 512, 16))
    for p in range(k // 512):
        a[p, :8] = np.random.permutation(np.resize(levels, 8))
        for g in range(8):
            far = levels[np.abs(levels - a[p, g]) >= 10]
            a[p, g + 8] = far[np.random.randint(len(far))]
    return np.exp2(a.ravel()).repeat(32)


def f64(x):
    return np.asarray(x).astype(np.float64)


def striped(idx):
    return np.tile(idx.reshape(-1, 16).T, (8, 1)).astype(np.uint16)


def unstriped(offs):
    return offs[:16].T.reshape(-1).astype(np.int64)


def pack_weight(w):
    k, n = w.shape
    w = f64(np.asarray(w, np.float32).astype(ml_dtypes.bfloat16)).reshape(k // 32, 32, n)
    amax = np.abs(w).max(1)
    byte = np.clip(np.where(amax > 0, np.frexp(amax)[1] - 1 + 127 - 7, 1), 1, 254)
    scaled = (w * np.exp2(127.0 - byte)[:, None, :]).reshape(k, n).astype(np.float32)
    words = np.ascontiguousarray(scaled.reshape(k // 512, 128, 4, n).transpose(0, 1, 3, 2)).astype(ml_dtypes.float8_e4m3fn).view(np.uint8)
    return words, np.ascontiguousarray(byte.astype(np.uint8).reshape(k // 512, 16, n))


def unpack_weight(words, scales):
    g, p, n, _ = words.shape
    vals = np.ascontiguousarray(words).view(ml_dtypes.float8_e4m3fn).astype(np.float64) * np.repeat(np.exp2(scales.astype(np.float64) - 127.0), 8, axis=1)[..., None]
    return vals.transpose(0, 1, 3, 2).reshape(g * 512, n)


K, T, S, V, N = 1024, 2048, 1024, 512, 256
P = 2 ** 7


def setup_inputs():
    n = np.random.standard_normal
    s = mx_kscale(K)[:, None]
    packed_w1 = pack_weight(n((K, N)) / np.sqrt(K) / s)
    return {
        "xT": (n((K, T)) * s).astype(np.float32),
        "w1_words": packed_w1[0],
        "w1_scales": packed_w1[1],
        "fx": np.tile(np.random.uniform(0.05, 0.95, V), (P, 1)).astype(np.float32),
        "fy": np.tile(np.random.uniform(0.05, 0.95, V), (P, 1)).astype(np.float32),
        "offs": striped(np.random.permutation(T)[:S]),
        "c00": striped(np.random.permutation(S)[:V]),
        "c01": striped(np.random.permutation(S)[:V]),
        "c10": striped(np.random.permutation(S)[:V]),
        "c11": striped(np.random.permutation(S)[:V]),
    }


def reference(xT, w1_words, w1_scales, fx, fy, offs, c00, c01, c10, c11):
    xq = mxq(f64(xT)[:, unstriped(offs)], 0, "e4m3")
    y = unpack_weight(w1_words, w1_scales).T @ xq
    top = y[:, unstriped(c00)] + (y[:, unstriped(c01)] - y[:, unstriped(c00)]) * f64(fx)[:1]
    low = y[:, unstriped(c10)] + (y[:, unstriped(c11)] - y[:, unstriped(c10)]) * f64(fx)[:1]
    return top + (low - top) * f64(fy)[:1]

@@ -1,0 +1,215 @@
+from contextlib import ExitStack
+
+import concourse.mybir as mybir
+from concourse.masks import make_identity
+
+K, T, S, V, N = 1024, 2048, 1024, 512, 256
+P = 128
+FLOPS = 2 * K * N * S
+
+F32 = mybir.dt.float32
+BF16 = mybir.dt.bfloat16
+U32 = mybir.dt.uint32
+I32 = mybir.dt.int32
+U16 = mybir.dt.uint16
+U8 = mybir.dt.uint8
+FP8X4 = mybir.dt.float8_e4m3fn_x4
+COPY = mybir.ActivationFunctionType.Copy
+MULT = mybir.AluOpType.mult
+ADD = mybir.AluOpType.add
+
+PIECES = ((0, 512), (512, 768), (768, 1024))
+VECTOR_PIECE = 2
+PAIR_CHUNKS = ((1024, 1024), (512, 512, 512, 512), (512, 512, 512, 512))
+LAST_CHUNKS = (512, 512, 512, 256, 256)
+
+
+def tile_picked_bilin_none_e_kernel(
+    tc, xT, w1_words, w1_scales, fx, fy, offs, c00, c01, c10, c11, out
+):
+    nc = tc.nc
+    with ExitStack() as ctx:
+        keep = ctx.enter_context(tc.tile_pool(name="keep", bufs=1))
+        psum = ctx.enter_context(tc.psum_pool(name="psum", bufs=1))
+
+        def rows(z):
+            return xT[512 * z : 512 * (z + 1), :].rearrange("(p j) t -> p j t", j=4)
+
+        def entries(lst, lo, hi):
+            return lst[:, lo // 16 : hi // 16]
+
+        ident = keep.tile([P, P], F32, name="ident")
+        frac_rows = keep.tile([P, P], F32, name="frac_rows")
+        w_scale = keep.tile([P, N], U8, name="w_scale", align_bytes=64)
+        nc.gpsimd.memset(frac_rows[:], 0.0)
+        nc.gpsimd.memset(w_scale[:].bitcast(I32), 0)
+        make_identity(nc, ident[:])
+
+        plane_first = keep.tile([P, T], F32, name="plane_first")
+        nc.sync.dma_start(plane_first[:], rows(1)[:, 2, :])
+        picked = keep.tile([P, S // 16], U16, name="picked")
+        nc.sync.dma_start(picked[:], offs)
+        nc.sync.dma_start(frac_rows[0:4, :], fx[0:1, :].rearrange("o (c p) -> (o c) p", p=P))
+        nc.sync.dma_start(frac_rows[4:8, :], fy[0:1, :].rearrange("o (c p) -> (o c) p", p=P))
+
+        raw = []
+        for i, (z, u) in enumerate(((0, 0), (0, 1), (1, 0))):
+            chunks, lo = [], 0
+            for j, width in enumerate(PAIR_CHUNKS[i]):
+                chunk = keep.tile([P, 2, width], F32, name=f"raw{i}_{j}")
+                nc.sync.dma_start(chunk[:], rows(z)[:, 2 * u : 2 * u + 2, lo : lo + width])
+                chunks.append((chunk, lo, width))
+                lo = lo + width
+            raw.append(chunks)
+            if i == 0:
+                for q in range(4):
+                    nc.sync.dma_start(
+                        w_scale[32 * q : 32 * q + 8, :].bitcast(I32), w1_scales[:, 4 * q : 4 * q + 4, :].bitcast(I32)
+                    )
+        plane_last = keep.tile([P, T], F32, name="plane_last")
+        lo = 0
+        for width in LAST_CHUNKS:
+            nc.sync.dma_start(plane_last[:, lo : lo + width], rows(1)[:, 3, lo : lo + width])
+            lo = lo + width
+        w_words = []
+        for z in range(2):
+            words = keep.tile([P, N], U32, name=f"w_words{z}", align_bytes=64)
+            nc.sync.dma_start(words[:].bitcast(I32), w1_words[z].rearrange("p n t -> p (n t)").bitcast(I32))
+            w_words.append(words)
+        corner = []
+        for i, lst in enumerate((c00, c01, c10, c11)):
+            tile = keep.tile([P, V // 16], U16, name=f"corner{i}")
+            nc.sync.dma_start(tile[:], lst)
+            corner.append(tile)
+
+        frac_ps = psum.tile([P, 512], F32, name="frac_ps", tag="acc0")
+        nc.tensor.transpose(frac_ps[:, 0:P], frac_rows[:], ident[:])
+        frac = keep.tile([P, 8], F32, name="frac")
+        nc.scalar.activation(frac[:], frac_ps[:, 0:8], COPY)
+        rest = keep.tile([P, 8], F32, name="rest")
+        nc.vector.tensor_scalar(rest[:], frac[:], -1.0, 1.0, MULT, ADD)
+        weight = keep.tile([P, 16], F32, name="weight")
+        for i in range(4):
+            along_x = frac if i % 2 else rest
+            along_y = frac if i // 2 else rest
+            nc.vector.tensor_tensor(weight[:, 4 * i : 4 * i + 4], along_x[:, 0:4], along_y[:, 4:8], MULT)
+        spread_ps = psum.tile([P, V], F32, name="spread_ps", tag="acc1")
+        for c in range(4):
+            nc.tensor.transpose(spread_ps[:, c * P : (c + 1) * P], weight[:, 12 + c : 13 + c].to_broadcast([P, P]), ident[:])
+        w11 = keep.tile([P, V], F32, name="w11")
+        nc.scalar.activation(w11[:], spread_ps[:], COPY)
+
+        grouped0 = keep.tile([P, 4 * S], BF16, name="grouped0", align_bytes=64)
+        grouped1 = [
+            keep.tile([P, 4 * (hi - lo)], BF16, name=f"grouped1_{i}", align_bytes=64) for i, (lo, hi) in enumerate(PIECES)
+        ]
+        for i, (lo, hi) in enumerate(PIECES):
+            nc.vector.tensor_copy(grouped1[i][:, 2 : 4 * (hi - lo) : 4], plane_first[:].indirect(entries(picked, lo, hi)))
+
+        def cast_pair(i):
+            pair = keep.tile([P, 2 * T], BF16, name=f"pair{i}", tag=f"pair{i}")
+            for j, (chunk, lo, width) in enumerate(raw[i]):
+                cut = width if j + 1 < len(raw[i]) else 3 * width // 8
+                src = chunk[:].rearrange("p u c -> p c u")
+                dst = pair[:, 2 * lo : 2 * (lo + width)].rearrange("p (c u) -> p c u", u=2)
+                nc.scalar.activation(dst[:, 0:cut, :], src[:, 0:cut, :], COPY)
+                if cut < width:
+                    nc.vector.tensor_copy(dst[:, cut:width, :], src[:, cut:width, :])
+            return pair[:].bitcast(U32)
+
+        for u in range(2):
+            window = cast_pair(u)
+            nc.vector.tensor_copy(grouped0[:].bitcast(U32)[:, u : 2 * S : 2], window.indirect(picked[:]))
+        codes0 = keep.tile([P, S], U32, name="codes0", align_bytes=64)
+        scale0 = keep.tile([P, S], U8, name="scale0", align_bytes=64)
+        for lo in range(0, S, 512):
+            nc.vector.quantize_mx(
+                out=codes0[:, lo : lo + 512].bitcast(FP8X4),
+                scales=scale0[:, lo : lo + 512],
+                in_=grouped0[:, 4 * lo : 4 * (lo + 512)],
+            )
+        window = cast_pair(2)
+        for i, (lo, hi) in enumerate(PIECES):
+            nc.vector.tensor_copy(
+                grouped1[i][:].bitcast(U32)[:, 0 : 2 * (hi - lo) : 2], window.indirect(entries(picked, lo, hi))
+            )
+        last_bf = keep.tile([P, T], BF16, name="last_bf", tag="pair0")
+        lo = 0
+        for width in LAST_CHUNKS:
+            nc.scalar.activation(last_bf[:, lo : lo + width], plane_last[:, lo : lo + width], COPY)
+            lo = lo + width
+        for i, (lo, hi) in enumerate(PIECES):
+            dst = grouped1[i][:, 3 : 4 * (hi - lo) : 4]
+            if i == VECTOR_PIECE:
+                nc.vector.tensor_copy(dst, plane_last[:].indirect(entries(picked, lo, hi)))
+            else:
+                nc.scalar.activation(dst, last_bf[:].indirect(entries(picked, lo, hi)), COPY)
+
+        banks = {}
+        for i, (lo, hi) in enumerate(PIECES):
+            for b in range(2):
+                bank = psum.tile([P, 512], F32, name=f"y_ps{i}_{b}", tag=f"bank{i}_{b}")
+                banks[i, b] = bank
+                nc.tensor.matmul_mx(
+                    out=bank[:, 0 : hi - lo],
+                    lhsT=w_words[0][:, b * P : (b + 1) * P].bitcast(FP8X4),
+                    lhsT_scale=w_scale[:, b * P : (b + 1) * P],
+                    rhs=codes0[:, lo:hi].bitcast(FP8X4),
+                    rhs_scale=scale0[:, lo:hi],
+                    start=True,
+                    stop=False,
+                )
+        y = [keep.tile([P, S], F32, name=f"y{b}") for b in range(2)]
+        for i in (0, 2, 1):
+            lo, hi = PIECES[i]
+            codes1 = keep.tile([P, hi - lo], U32, name=f"codes1_{i}", align_bytes=64)
+            scale1 = keep.tile([P, hi - lo], U8, name=f"scale1_{i}", align_bytes=64)
+            nc.vector.quantize_mx(out=codes1[:].bitcast(FP8X4), scales=scale1[:], in_=grouped1[i][:])
+            for b in range(2):
+                nc.tensor.matmul_mx(
+                    out=banks[i, b][:, 0 : hi - lo],
+                    lhsT=w_words[1][:, b * P : (b + 1) * P].bitcast(FP8X4),
+                    lhsT_scale=w_scale[4:P, b * P : (b + 1) * P],
+                    rhs=codes1[:].bitcast(FP8X4),
+                    rhs_scale=scale1[:],
+                    start=False,
+                    stop=True,
+                )
+        for b in range(2):
+            for i in (0, 2, 1):
+                lo, hi = PIECES[i]
+                if b == 0 and i > 0:
+                    nc.vector.tensor_copy(y[b][:, lo:hi], banks[i, b][:, 0 : hi - lo])
+                else:
+                    nc.scalar.activation(y[b][:, lo:hi], banks[i, b][:, 0 : hi - lo], COPY)
+
+        for b in range(2):
+            acc = psum.tile([P, V], F32, name=f"acc{b}", tag=f"acc{b}")
+            for i in range(3):
+                got = keep.tile([P, V], F32, name=f"got{i}_{b}")
+                nc.vector.tensor_copy(got[:], y[b][:].indirect(corner[i][:]))
+                turned = psum.tile([P, V], F32, name=f"turned{i}_{b}", tag=f"bank{i}_{b}")
+                for c in range(4):
+                    nc.tensor.transpose(turned[:, c * P : (c + 1) * P], got[:, c * P : (c + 1) * P], ident[:])
+                scaled = keep.tile([P, V], F32, name=f"scaled{i}_{b}")
+                for c in range(4):
+                    nc.scalar.activation(
+                        scaled[:, c * P : (c + 1) * P],
+                        turned[:, c * P : (c + 1) * P],
+                        COPY,
+                        scale=weight[:, 4 * i + c : 4 * i + c + 1],
+                    )
+                for c in range(4):
+                    nc.tensor.matmul(
+                        acc[:, c * P : (c + 1) * P],
+                        scaled[:, c * P : (c + 1) * P],
+                        ident[:],
+                        start=(i == 0 and c == 0),
+                        stop=(i == 2 and c == 3),
+                        is_transpose=True,
+                    )
+            fourth = keep.tile([P, V], F32, name=f"fourth{b}", tag="fourth")
+            nc.vector.tensor_tensor(fourth[:], y[b][:].indirect(corner[3][:]), w11[:], MULT)
+            result = keep.tile([P, V], F32, name=f"result{b}")
+            nc.vector.tensor_tensor(result[:], fourth[:], acc[:], ADD)
+            nc.sync.dma_start(out[b * P : (b + 1) * P, :], result[:])

@@ -18,10 +18,13 @@ COPY = mybir.ActivationFunctionType.Copy
 MULT = mybir.AluOpType.mult
 ADD = mybir.AluOpType.add
 
-PIECES = ((0, 512), (512, 768), (768, 1024))
-VECTOR_PIECE = 2
-PAIR_CHUNKS = ((1024, 1024), (512, 512, 512, 512), (512, 512, 512, 512))
-LAST_CHUNKS = (512, 512, 512, 256, 256)
+PIECE = 256
+PAIR_CHUNKS = (
+    ((1024, 0), (512, 512), (512, 512)),
+    ((1024, 1024), (512, 0), (512, 192)),
+    ((768, 768), (768, 768), (512, 256)),
+    ((768, 768), (768, 768), (256, 0), (256, 0)),
+)
 
 
 def tile_picked_bilin_none_e_kernel(
@@ -45,47 +48,39 @@ def tile_picked_bilin_none_e_kernel(
         nc.gpsimd.memset(w_scale[:].bitcast(I32), 0)
         make_identity(nc, ident[:])
 
-        plane_first = keep.tile([P, T], F32, name="plane_first")
-        nc.sync.dma_start(plane_first[:], rows(1)[:, 2, :])
         picked = keep.tile([P, S // 16], U16, name="picked")
-        nc.sync.dma_start(picked[:], offs)
-        nc.sync.dma_start(frac_rows[0:4, :], fx[0:1, :].rearrange("o (c p) -> (o c) p", p=P))
-        nc.sync.dma_start(frac_rows[4:8, :], fy[0:1, :].rearrange("o (c p) -> (o c) p", p=P))
-
         raw = []
-        for i, (z, u) in enumerate(((0, 0), (0, 1), (1, 0))):
+        for i in range(4):
             chunks, lo = [], 0
-            for j, width in enumerate(PAIR_CHUNKS[i]):
+            for j, (width, cut) in enumerate(PAIR_CHUNKS[i]):
                 chunk = keep.tile([P, 2, width], F32, name=f"raw{i}_{j}")
-                nc.sync.dma_start(chunk[:], rows(z)[:, 2 * u : 2 * u + 2, lo : lo + width])
-                chunks.append((chunk, lo, width))
+                nc.sync.dma_start(chunk[:], rows(i // 2)[:, 2 * (i % 2) : 2 * (i % 2) + 2, lo : lo + width])
+                chunks.append((chunk, lo, width, cut))
                 lo = lo + width
+                if (i, j) == (0, 0):
+                    nc.sync.dma_start(picked[:], offs)
+                    nc.sync.dma_start(frac_rows[0:4, :], fx[0:1, :].rearrange("o (c p) -> (o c) p", p=P))
+                    nc.sync.dma_start(frac_rows[4:8, :], fy[0:1, :].rearrange("o (c p) -> (o c) p", p=P))
+                if (i, j) == (1, 0):
+                    for q in range(4):
+                        nc.sync.dma_start(
+                            w_scale[32 * q : 32 * q + 8, :].bitcast(I32),
+                            w1_scales[:, 4 * q : 4 * q + 4, :].bitcast(I32),
+                        )
             raw.append(chunks)
-            if i == 0:
-                for q in range(4):
-                    nc.sync.dma_start(
-                        w_scale[32 * q : 32 * q + 8, :].bitcast(I32), w1_scales[:, 4 * q : 4 * q + 4, :].bitcast(I32)
-                    )
-        plane_last = keep.tile([P, T], F32, name="plane_last")
-        lo = 0
-        for width in LAST_CHUNKS:
-            nc.sync.dma_start(plane_last[:, lo : lo + width], rows(1)[:, 3, lo : lo + width])
-            lo = lo + width
-        w_words = []
+        w_words = [keep.tile([P, N], U32, name=f"w_words{z}", align_bytes=64) for z in range(2)]
         for z in range(2):
-            words = keep.tile([P, N], U32, name=f"w_words{z}", align_bytes=64)
-            nc.sync.dma_start(words[:].bitcast(I32), w1_words[z].rearrange("p n t -> p (n t)").bitcast(I32))
-            w_words.append(words)
+            nc.sync.dma_start(w_words[z][:].bitcast(I32), w1_words[z].rearrange("p n t -> p (n t)").bitcast(I32))
         corner = []
         for i, lst in enumerate((c00, c01, c10, c11)):
             tile = keep.tile([P, V // 16], U16, name=f"corner{i}")
             nc.sync.dma_start(tile[:], lst)
             corner.append(tile)
 
-        frac_ps = psum.tile([P, 512], F32, name="frac_ps", tag="acc0")
+        frac_ps = psum.tile([P, 512], F32, name="frac_ps", tag="bank2_0")
         nc.tensor.transpose(frac_ps[:, 0:P], frac_rows[:], ident[:])
         frac = keep.tile([P, 8], F32, name="frac")
-        nc.scalar.activation(frac[:], frac_ps[:, 0:8], COPY)
+        nc.vector.tensor_copy(frac[:], frac_ps[:, 0:8])
         rest = keep.tile([P, 8], F32, name="rest")
         nc.vector.tensor_scalar(rest[:], frac[:], -1.0, 1.0, MULT, ADD)
         weight = keep.tile([P, 16], F32, name="weight")
@@ -93,81 +88,63 @@ def tile_picked_bilin_none_e_kernel(
             along_x = frac if i % 2 else rest
             along_y = frac if i // 2 else rest
             nc.vector.tensor_tensor(weight[:, 4 * i : 4 * i + 4], along_x[:, 0:4], along_y[:, 4:8], MULT)
-        spread_ps = psum.tile([P, V], F32, name="spread_ps", tag="acc1")
+        spread_ps = psum.tile([P, V], F32, name="spread_ps", tag="bank3_0")
         for c in range(4):
             nc.tensor.transpose(spread_ps[:, c * P : (c + 1) * P], weight[:, 12 + c : 13 + c].to_broadcast([P, P]), ident[:])
         w11 = keep.tile([P, V], F32, name="w11")
-        nc.scalar.activation(w11[:], spread_ps[:], COPY)
-
-        grouped0 = keep.tile([P, 4 * S], BF16, name="grouped0", align_bytes=64)
-        grouped1 = [
-            keep.tile([P, 4 * (hi - lo)], BF16, name=f"grouped1_{i}", align_bytes=64) for i, (lo, hi) in enumerate(PIECES)
-        ]
-        for i, (lo, hi) in enumerate(PIECES):
-            nc.vector.tensor_copy(grouped1[i][:, 2 : 4 * (hi - lo) : 4], plane_first[:].indirect(entries(picked, lo, hi)))
+        nc.vector.tensor_copy(w11[:], spread_ps[:])
 
         def cast_pair(i):
-            pair = keep.tile([P, 2 * T], BF16, name=f"pair{i}", tag=f"pair{i}")
-            for j, (chunk, lo, width) in enumerate(raw[i]):
-                cut = width if j + 1 < len(raw[i]) else 3 * width // 8
+            pair = keep.tile([P, 2 * T], BF16, name=f"pair{i}")
+            for chunk, lo, width, cut in raw[i]:
                 src = chunk[:].rearrange("p u c -> p c u")
                 dst = pair[:, 2 * lo : 2 * (lo + width)].rearrange("p (c u) -> p c u", u=2)
-                nc.scalar.activation(dst[:, 0:cut, :], src[:, 0:cut, :], COPY)
+                if cut > 0:
+                    nc.scalar.activation(dst[:, 0:cut, :], src[:, 0:cut, :], COPY)
                 if cut < width:
                     nc.vector.tensor_copy(dst[:, cut:width, :], src[:, cut:width, :])
             return pair[:].bitcast(U32)
 
+        pieces = range(S // PIECE)
+        grouped0 = keep.tile([P, 4 * S], BF16, name="grouped0", align_bytes=64)
         for u in range(2):
-            window = cast_pair(u)
-            nc.vector.tensor_copy(grouped0[:].bitcast(U32)[:, u : 2 * S : 2], window.indirect(picked[:]))
+            nc.vector.tensor_copy(grouped0[:].bitcast(U32)[:, u : 2 * S : 2], cast_pair(u).indirect(picked[:]))
         codes0 = keep.tile([P, S], U32, name="codes0", align_bytes=64)
         scale0 = keep.tile([P, S], U8, name="scale0", align_bytes=64)
-        for lo in range(0, S, 512):
-            nc.vector.quantize_mx(
-                out=codes0[:, lo : lo + 512].bitcast(FP8X4),
-                scales=scale0[:, lo : lo + 512],
-                in_=grouped0[:, 4 * lo : 4 * (lo + 512)],
-            )
-        window = cast_pair(2)
-        for i, (lo, hi) in enumerate(PIECES):
-            nc.vector.tensor_copy(
-                grouped1[i][:].bitcast(U32)[:, 0 : 2 * (hi - lo) : 2], window.indirect(entries(picked, lo, hi))
-            )
-        last_bf = keep.tile([P, T], BF16, name="last_bf", tag="pair0")
-        lo = 0
-        for width in LAST_CHUNKS:
-            nc.scalar.activation(last_bf[:, lo : lo + width], plane_last[:, lo : lo + width], COPY)
-            lo = lo + width
-        for i, (lo, hi) in enumerate(PIECES):
-            dst = grouped1[i][:, 3 : 4 * (hi - lo) : 4]
-            if i == VECTOR_PIECE:
-                nc.vector.tensor_copy(dst, plane_last[:].indirect(entries(picked, lo, hi)))
-            else:
-                nc.scalar.activation(dst, last_bf[:].indirect(entries(picked, lo, hi)), COPY)
+        nc.vector.quantize_mx(out=codes0[:].bitcast(FP8X4), scales=scale0[:], in_=grouped0[:])
+
+        halves1 = [keep.tile([P, 2, PIECE], U32, name=f"halves1_{i}") for i in pieces]
+        for u in range(2):
+            window = cast_pair(2 + u)
+            for i in pieces:
+                nc.vector.tensor_copy(halves1[i][:, u, :], window.indirect(entries(picked, i * PIECE, (i + 1) * PIECE)))
 
         banks = {}
-        for i, (lo, hi) in enumerate(PIECES):
-            for b in range(2):
+        for b in range(2):
+            for i in pieces:
                 bank = psum.tile([P, 512], F32, name=f"y_ps{i}_{b}", tag=f"bank{i}_{b}")
                 banks[i, b] = bank
                 nc.tensor.matmul_mx(
-                    out=bank[:, 0 : hi - lo],
+                    out=bank[:, 0:PIECE],
                     lhsT=w_words[0][:, b * P : (b + 1) * P].bitcast(FP8X4),
                     lhsT_scale=w_scale[:, b * P : (b + 1) * P],
-                    rhs=codes0[:, lo:hi].bitcast(FP8X4),
-                    rhs_scale=scale0[:, lo:hi],
+                    rhs=codes0[:, i * PIECE : (i + 1) * PIECE].bitcast(FP8X4),
+                    rhs_scale=scale0[:, i * PIECE : (i + 1) * PIECE],
                     start=True,
                     stop=False,
                 )
         y = [keep.tile([P, S], F32, name=f"y{b}") for b in range(2)]
-        for i in (0, 2, 1):
-            lo, hi = PIECES[i]
-            codes1 = keep.tile([P, hi - lo], U32, name=f"codes1_{i}", align_bytes=64)
-            scale1 = keep.tile([P, hi - lo], U8, name=f"scale1_{i}", align_bytes=64)
-            nc.vector.quantize_mx(out=codes1[:].bitcast(FP8X4), scales=scale1[:], in_=grouped1[i][:])
+        for i in pieces:
+            grouped1 = keep.tile([P, 4 * PIECE], BF16, name=f"grouped1_{i}", align_bytes=64)
+            nc.scalar.copy(
+                grouped1[:].bitcast(U32).rearrange("p (n u) -> p n u", u=2), halves1[i][:].rearrange("p u n -> p n u")
+            )
+            codes1 = keep.tile([P, PIECE], U32, name=f"codes1_{i}", align_bytes=64)
+            scale1 = keep.tile([P, PIECE], U8, name=f"scale1_{i}", align_bytes=64)
+            nc.vector.quantize_mx(out=codes1[:].bitcast(FP8X4), scales=scale1[:], in_=grouped1[:])
             for b in range(2):
                 nc.tensor.matmul_mx(
-                    out=banks[i, b][:, 0 : hi - lo],
+                    out=banks[i, b][:, 0:PIECE],
                     lhsT=w_words[1][:, b * P : (b + 1) * P].bitcast(FP8X4),
                     lhsT_scale=w_scale[4:P, b * P : (b + 1) * P],
                     rhs=codes1[:].bitcast(FP8X4),
@@ -176,19 +153,20 @@ def tile_picked_bilin_none_e_kernel(
                     stop=True,
                 )
         for b in range(2):
-            for i in (0, 2, 1):
-                lo, hi = PIECES[i]
-                if b == 0 and i > 0:
-                    nc.vector.tensor_copy(y[b][:, lo:hi], banks[i, b][:, 0 : hi - lo])
+            for i in pieces:
+                if b == 0 and i == len(pieces) - 1:
+                    nc.vector.tensor_copy(y[b][:, i * PIECE : (i + 1) * PIECE], banks[i, b][:, 0:PIECE])
                 else:
-                    nc.scalar.activation(y[b][:, lo:hi], banks[i, b][:, 0 : hi - lo], COPY)
+                    nc.scalar.activation(y[b][:, i * PIECE : (i + 1) * PIECE], banks[i, b][:, 0:PIECE], COPY)
 
+        accs = []
         for b in range(2):
-            acc = psum.tile([P, V], F32, name=f"acc{b}", tag=f"acc{b}")
+            acc = psum.tile([P, V], F32, name=f"acc{b}", tag=f"bank{2 + b}_0")
+            accs.append(acc)
             for i in range(3):
-                got = keep.tile([P, V], F32, name=f"got{i}_{b}")
+                got = keep.tile([P, V], F32, name=f"got{i}_{b}", tag=f"got{i}_{b}")
                 nc.vector.tensor_copy(got[:], y[b][:].indirect(corner[i][:]))
-                turned = psum.tile([P, V], F32, name=f"turned{i}_{b}", tag=f"bank{i}_{b}")
+                turned = psum.tile([P, V], F32, name=f"turned{i}_{b}", tag=f"bank{(3 * b + i) % 2}_0")
                 for c in range(4):
                     nc.tensor.transpose(turned[:, c * P : (c + 1) * P], got[:, c * P : (c + 1) * P], ident[:])
                 scaled = keep.tile([P, V], F32, name=f"scaled{i}_{b}")
@@ -208,8 +186,13 @@ def tile_picked_bilin_none_e_kernel(
                         stop=(i == 2 and c == 3),
                         is_transpose=True,
                     )
-            fourth = keep.tile([P, V], F32, name=f"fourth{b}", tag="fourth")
-            nc.vector.tensor_tensor(fourth[:], y[b][:].indirect(corner[3][:]), w11[:], MULT)
+        for b in range(2):
+            acc = accs[b]
+            fourth = keep.tile([P, V], F32, name=f"fourth{b}", tag="got0_1")
             result = keep.tile([P, V], F32, name=f"result{b}")
-            nc.vector.tensor_tensor(result[:], fourth[:], acc[:], ADD)
-            nc.sync.dma_start(out[b * P : (b + 1) * P, :], result[:])
+            parts = ((0, V),) if b == 0 else ((0, V // 2), (V // 2, V))
+            for lo, hi in parts:
+                nc.vector.tensor_tensor(fourth[:, lo:hi], y[b][:].indirect(entries(corner[3], lo, hi)), w11[:, lo:hi], MULT)
+            for lo, hi in parts:
+                nc.vector.tensor_tensor(result[:, lo:hi], fourth[:, lo:hi], acc[:, lo:hi], ADD)
+                nc.sync.dma_start(out[b * P : (b + 1) * P, lo:hi], result[:, lo:hi])

@@ -23,7 +23,7 @@ PAIR_CHUNKS = (
     ((1024, 0), (512, 512), (512, 512)),
     ((1024, 1024), (512, 0), (512, 192)),
     ((768, 768), (768, 768), (512, 256)),
-    ((768, 768), (768, 768), (256, 0), (256, 0)),
+    ((768, 768), (512, 512), (512, 0), (256, 128)),
 )
 
 
@@ -61,16 +61,15 @@ def tile_picked_bilin_none_e_kernel(
                     nc.sync.dma_start(picked[:], offs)
                     nc.sync.dma_start(frac_rows[0:4, :], fx[0:1, :].rearrange("o (c p) -> (o c) p", p=P))
                     nc.sync.dma_start(frac_rows[4:8, :], fy[0:1, :].rearrange("o (c p) -> (o c) p", p=P))
-                if (i, j) == (1, 0):
-                    for q in range(4):
-                        nc.sync.dma_start(
-                            w_scale[32 * q : 32 * q + 8, :].bitcast(I32),
-                            w1_scales[:, 4 * q : 4 * q + 4, :].bitcast(I32),
-                        )
             raw.append(chunks)
         w_words = [keep.tile([P, N], U32, name=f"w_words{z}", align_bytes=64) for z in range(2)]
         for z in range(2):
             nc.sync.dma_start(w_words[z][:].bitcast(I32), w1_words[z].rearrange("p n t -> p (n t)").bitcast(I32))
+            if z == 0:
+                for q in range(4):
+                    nc.sync.dma_start(
+                        w_scale[32 * q : 32 * q + 8, :].bitcast(I32), w1_scales[:, 4 * q : 4 * q + 4, :].bitcast(I32)
+                    )
         corner = []
         for i, lst in enumerate((c00, c01, c10, c11)):
             tile = keep.tile([P, V // 16], U16, name=f"corner{i}")

@@ -20,7 +20,7 @@ ADD = mybir.AluOpType.add
 
 PIECE = 256
 PAIR_CHUNKS = (
-    ((1024, 0), (512, 512), (512, 512)),
+    ((1024, 0), (512, 512), (512, 192)),
     ((1024, 1024), (512, 0), (512, 192)),
     ((768, 768), (768, 768), (512, 256)),
     ((768, 768), (512, 512), (512, 0), (256, 128)),
@@ -78,23 +78,32 @@ def tile_picked_bilin_none_e_kernel(
 
         frac_ps = psum.tile([P, 512], F32, name="frac_ps", tag="bank2_0")
         nc.tensor.transpose(frac_ps[:, 0:P], frac_rows[:], ident[:])
-        frac = keep.tile([P, 8], F32, name="frac")
-        nc.vector.tensor_copy(frac[:], frac_ps[:, 0:8])
-        rest = keep.tile([P, 8], F32, name="rest")
-        nc.vector.tensor_scalar(rest[:], frac[:], -1.0, 1.0, MULT, ADD)
+        sides = keep.tile([P, 2, 8], F32, name="sides")
+        nc.vector.tensor_scalar(sides[:, 0, :], frac_ps[:, 0:8], -1.0, 1.0, MULT, ADD)
+        nc.vector.tensor_copy(sides[:, 1, :], frac_ps[:, 0:8])
         weight = keep.tile([P, 16], F32, name="weight")
-        for i in range(4):
-            along_x = frac if i % 2 else rest
-            along_y = frac if i // 2 else rest
-            nc.vector.tensor_tensor(weight[:, 4 * i : 4 * i + 4], along_x[:, 0:4], along_y[:, 4:8], MULT)
+        nc.gpsimd.tensor_tensor(
+            weight[:].rearrange("p (j i c) -> p j i c", j=2, i=2),
+            sides[:, :, 0:4].unsqueeze(1).to_broadcast([P, 2, 2, 4]),
+            sides[:, :, 4:8].unsqueeze(2).to_broadcast([P, 2, 2, 4]),
+            MULT,
+        )
         spread_ps = psum.tile([P, V], F32, name="spread_ps", tag="bank3_0")
         for c in range(4):
             nc.tensor.transpose(spread_ps[:, c * P : (c + 1) * P], weight[:, 12 + c : 13 + c].to_broadcast([P, P]), ident[:])
-        w11 = keep.tile([P, V], F32, name="w11")
-        nc.vector.tensor_copy(w11[:], spread_ps[:])
+
+        late1, late2, late3 = 1024, 256, 768
+        first = keep.tile([P, 2 * (2 * T - late1)], BF16, name="first", align_bytes=64)
+        second = keep.tile([P, 2 * (2 * T - late3 - late2 + 2 * S)], BF16, name="second", align_bytes=64)
+        pairs = [
+            first[:, 2 * (T - late1) : 2 * (2 * T - late1)],
+            first[:, 0 : 2 * T],
+            second[:, 2 * (T - late3) : 2 * (2 * T - late3)],
+            second[:, 0 : 2 * T],
+        ]
 
         def cast_pair(i):
-            pair = keep.tile([P, 2 * T], BF16, name=f"pair{i}")
+            pair = pairs[i]
             for chunk, lo, width, cut in raw[i]:
                 src = chunk[:].rearrange("p u c -> p c u")
                 dst = pair[:, 2 * lo : 2 * (lo + width)].rearrange("p (c u) -> p c u", u=2)
@@ -102,15 +111,17 @@ def tile_picked_bilin_none_e_kernel(
                     nc.scalar.activation(dst[:, 0:cut, :], src[:, 0:cut, :], COPY)
                 if cut < width:
                     nc.vector.tensor_copy(dst[:, cut:width, :], src[:, cut:width, :])
-            return pair[:].bitcast(U32)
+            return pair.bitcast(U32)
 
         pieces = range(S // PIECE)
-        grouped0 = keep.tile([P, 4 * S], BF16, name="grouped0", align_bytes=64)
+        grouped0 = second[:, 2 * (2 * T - late3 - late2) :]
         for u in range(2):
-            nc.vector.tensor_copy(grouped0[:].bitcast(U32)[:, u : 2 * S : 2], cast_pair(u).indirect(picked[:]))
+            nc.vector.tensor_copy(grouped0.bitcast(U32)[:, u : 2 * S : 2], cast_pair(u).indirect(picked[:]))
+        w11 = keep.tile([P, V], F32, name="w11")
+        nc.scalar.activation(w11[:], spread_ps[:], COPY)
         codes0 = keep.tile([P, S], U32, name="codes0", align_bytes=64)
         scale0 = keep.tile([P, S], U8, name="scale0", align_bytes=64)
-        nc.vector.quantize_mx(out=codes0[:].bitcast(FP8X4), scales=scale0[:], in_=grouped0[:])
+        nc.vector.quantize_mx(out=codes0[:].bitcast(FP8X4), scales=scale0[:], in_=grouped0)
 
         halves1 = [keep.tile([P, 2, PIECE], U32, name=f"halves1_{i}") for i in pieces]
         for u in range(2):

@@ -76,7 +76,7 @@ def tile_picked_bilin_none_e_kernel(
             nc.sync.dma_start(tile[:], lst)
             corner.append(tile)
 
-        frac_ps = psum.tile([P, 512], F32, name="frac_ps", tag="bank2_0")
+        frac_ps = psum.tile([P, 512], F32, name="frac_ps", tag="bank2")
         nc.tensor.transpose(frac_ps[:, 0:P], frac_rows[:], ident[:])
         sides = keep.tile([P, 2, 8], F32, name="sides")
         nc.vector.tensor_scalar(sides[:, 0, :], frac_ps[:, 0:8], -1.0, 1.0, MULT, ADD)
@@ -88,9 +88,13 @@ def tile_picked_bilin_none_e_kernel(
             sides[:, :, 4:8].unsqueeze(2).to_broadcast([P, 2, 2, 4]),
             MULT,
         )
-        spread_ps = psum.tile([P, V], F32, name="spread_ps", tag="bank3_0")
-        for c in range(4):
-            nc.tensor.transpose(spread_ps[:, c * P : (c + 1) * P], weight[:, 12 + c : 13 + c].to_broadcast([P, P]), ident[:])
+        spread_ps = []
+        for i in range(4):
+            bank = psum.tile([P, V], F32, name=f"spread_ps{i}", tag=("bank0", "bank1", "bank6", "bank7")[i])
+            spread_ps.append(bank)
+            for c in range(4):
+                column = weight[:, 4 * i + c : 4 * i + c + 1]
+                nc.tensor.transpose(bank[:, c * P : (c + 1) * P], column.to_broadcast([P, P]), ident[:])
 
         late1, late2, late3 = 1024, 256, 768
         first = keep.tile([P, 2 * (2 * T - late1)], BF16, name="first", align_bytes=64)
@@ -117,8 +121,9 @@ def tile_picked_bilin_none_e_kernel(
         grouped0 = second[:, 2 * (2 * T - late3 - late2) :]
         for u in range(2):
             nc.vector.tensor_copy(grouped0.bitcast(U32)[:, u : 2 * S : 2], cast_pair(u).indirect(picked[:]))
-        w11 = keep.tile([P, V], F32, name="w11")
-        nc.scalar.activation(w11[:], spread_ps[:], COPY)
+        upper = keep.tile([P, 2, V], F32, name="upper", tag="raw1_2")
+        for i in range(2):
+            nc.scalar.activation(upper[:, i, :], spread_ps[i][:], COPY)
         codes0 = keep.tile([P, S], U32, name="codes0", align_bytes=64)
         scale0 = keep.tile([P, S], U8, name="scale0", align_bytes=64)
         nc.vector.quantize_mx(out=codes0[:].bitcast(FP8X4), scales=scale0[:], in_=grouped0)
@@ -129,80 +134,85 @@ def tile_picked_bilin_none_e_kernel(
             for i in pieces:
                 nc.vector.tensor_copy(halves1[i][:, u, :], window.indirect(entries(picked, i * PIECE, (i + 1) * PIECE)))
 
-        banks = {}
-        for b in range(2):
-            for i in pieces:
-                bank = psum.tile([P, 512], F32, name=f"y_ps{i}_{b}", tag=f"bank{i}_{b}")
-                banks[i, b] = bank
-                nc.tensor.matmul_mx(
-                    out=bank[:, 0:PIECE],
-                    lhsT=w_words[0][:, b * P : (b + 1) * P].bitcast(FP8X4),
-                    lhsT_scale=w_scale[:, b * P : (b + 1) * P],
-                    rhs=codes0[:, i * PIECE : (i + 1) * PIECE].bitcast(FP8X4),
-                    rhs_scale=scale0[:, i * PIECE : (i + 1) * PIECE],
-                    start=True,
-                    stop=False,
-                )
-        y = [keep.tile([P, S], F32, name=f"y{b}") for b in range(2)]
-        for i in pieces:
-            grouped1 = keep.tile([P, 4 * PIECE], BF16, name=f"grouped1_{i}", align_bytes=64)
-            nc.scalar.copy(
-                grouped1[:].bitcast(U32).rearrange("p (n u) -> p n u", u=2), halves1[i][:].rearrange("p u n -> p n u")
+        def product(bank, b, z, codes, scale):
+            nc.tensor.matmul_mx(
+                out=bank,
+                lhsT=w_words[z][:, b * P : (b + 1) * P].bitcast(FP8X4),
+                lhsT_scale=w_scale[4 * z : P, b * P : (b + 1) * P],
+                rhs=codes.bitcast(FP8X4),
+                rhs_scale=scale,
+                start=(z == 0),
+                stop=(z == 1),
             )
-            codes1 = keep.tile([P, PIECE], U32, name=f"codes1_{i}", align_bytes=64)
-            scale1 = keep.tile([P, PIECE], U8, name=f"scale1_{i}", align_bytes=64)
-            nc.vector.quantize_mx(out=codes1[:].bitcast(FP8X4), scales=scale1[:], in_=grouped1[:])
-            for b in range(2):
-                nc.tensor.matmul_mx(
-                    out=banks[i, b][:, 0:PIECE],
-                    lhsT=w_words[1][:, b * P : (b + 1) * P].bitcast(FP8X4),
-                    lhsT_scale=w_scale[4:P, b * P : (b + 1) * P],
-                    rhs=codes1[:].bitcast(FP8X4),
-                    rhs_scale=scale1[:],
-                    start=False,
-                    stop=True,
+
+        banks0 = [psum.tile([P, 512], F32, name=f"y0_ps{i}", tag=f"bank{i}") for i in pieces]
+        banks1 = [psum.tile([P, 512], F32, name=f"y1_ps{h}", tag=f"bank{4 + h}") for h in range(2)]
+        for i in pieces:
+            cols = slice(i * PIECE, (i + 1) * PIECE)
+            product(banks0[i][:, 0:PIECE], 0, 0, codes0[:, cols], scale0[:, cols])
+        for h in range(2):
+            cols = slice(h * 512, (h + 1) * 512)
+            product(banks1[h][:], 1, 0, codes0[:, cols], scale0[:, cols])
+        y = [keep.tile([P, S], F32, name=f"y{b}") for b in range(2)]
+        made = []
+        for h in range(2):
+            codes1 = keep.tile([P, 512], U32, name=f"codes1_{h}", align_bytes=64)
+            scale1 = keep.tile([P, 512], U8, name=f"scale1_{h}", align_bytes=64)
+            made.append((codes1, scale1))
+            for j in range(2):
+                i = 2 * h + j
+                cols = slice(j * PIECE, (j + 1) * PIECE)
+                grouped1 = keep.tile([P, 4 * PIECE], BF16, name=f"grouped1_{i}", align_bytes=64)
+                nc.scalar.copy(
+                    grouped1[:].bitcast(U32).rearrange("p (n u) -> p n u", u=2), halves1[i][:].rearrange("p u n -> p n u")
                 )
-        for b in range(2):
-            for i in pieces:
-                if b == 0 and i == len(pieces) - 1:
-                    nc.vector.tensor_copy(y[b][:, i * PIECE : (i + 1) * PIECE], banks[i, b][:, 0:PIECE])
-                else:
-                    nc.scalar.activation(y[b][:, i * PIECE : (i + 1) * PIECE], banks[i, b][:, 0:PIECE], COPY)
+                nc.vector.quantize_mx(out=codes1[:, cols].bitcast(FP8X4), scales=scale1[:, cols], in_=grouped1[:])
+            for j in range(2):
+                cols = slice(j * PIECE, (j + 1) * PIECE)
+                product(banks0[2 * h + j][:, 0:PIECE], 0, 1, codes1[:, cols], scale1[:, cols])
+        for h in range(2):
+            product(banks1[h][:], 1, 1, made[h][0][:], made[h][1][:])
+        for i in pieces:
+            if i == len(pieces) - 1:
+                nc.vector.tensor_copy(y[0][:, i * PIECE : (i + 1) * PIECE], banks0[i][:, 0:PIECE])
+            else:
+                nc.scalar.activation(y[0][:, i * PIECE : (i + 1) * PIECE], banks0[i][:, 0:PIECE], COPY)
+        lower = keep.tile([P, 2, V], F32, name="lower", tag="codes1_1", align_bytes=64)
+        nc.scalar.activation(lower[:, 0, :], spread_ps[2][:], COPY)
+        for h in range(2):
+            nc.scalar.activation(y[1][:, h * 512 : (h + 1) * 512], banks1[h][:], COPY)
+        nc.scalar.activation(lower[:, 1, :], spread_ps[3][:], COPY)
+        spread = [upper[:, 0, :], upper[:, 1, :], lower[:, 0, :], lower[:, 1, :]]
 
         accs = []
         for b in range(2):
-            acc = psum.tile([P, V], F32, name=f"acc{b}", tag=f"bank{2 + b}_0")
-            accs.append(acc)
+            turned = psum.tile([P, V], F32, name=f"turned{b}", tag=f"bank{b}")
             for i in range(3):
                 got = keep.tile([P, V], F32, name=f"got{i}_{b}", tag=f"got{i}_{b}")
-                nc.vector.tensor_copy(got[:], y[b][:].indirect(corner[i][:]))
-                turned = psum.tile([P, V], F32, name=f"turned{i}_{b}", tag=f"bank{(3 * b + i) % 2}_0")
-                for c in range(4):
-                    nc.tensor.transpose(turned[:, c * P : (c + 1) * P], got[:, c * P : (c + 1) * P], ident[:])
-                scaled = keep.tile([P, V], F32, name=f"scaled{i}_{b}")
-                for c in range(4):
-                    nc.scalar.activation(
-                        scaled[:, c * P : (c + 1) * P],
-                        turned[:, c * P : (c + 1) * P],
-                        COPY,
-                        scale=weight[:, 4 * i + c : 4 * i + c + 1],
-                    )
+                nc.vector.tensor_tensor(got[:], y[b][:].indirect(corner[i][:]), spread[i], MULT)
                 for c in range(4):
                     nc.tensor.matmul(
-                        acc[:, c * P : (c + 1) * P],
-                        scaled[:, c * P : (c + 1) * P],
+                        turned[:, c * P : (c + 1) * P],
+                        got[:, c * P : (c + 1) * P],
                         ident[:],
                         start=(i == 0 and c == 0),
                         stop=(i == 2 and c == 3),
                         is_transpose=True,
                     )
+            three = keep.tile([P, V], F32, name=f"three{b}")
+            for h in range(2):
+                nc.scalar.activation(three[:, h * 256 : (h + 1) * 256], turned[:, h * 256 : (h + 1) * 256], COPY)
+            acc = psum.tile([P, V], F32, name=f"acc{b}", tag=f"bank{2 + b}")
+            accs.append(acc)
+            for c in range(4):
+                nc.tensor.transpose(acc[:, c * P : (c + 1) * P], three[:, c * P : (c + 1) * P], ident[:])
         for b in range(2):
             acc = accs[b]
             fourth = keep.tile([P, V], F32, name=f"fourth{b}", tag="got0_1")
             result = keep.tile([P, V], F32, name=f"result{b}")
             parts = ((0, V),) if b == 0 else ((0, V // 2), (V // 2, V))
             for lo, hi in parts:
-                nc.vector.tensor_tensor(fourth[:, lo:hi], y[b][:].indirect(entries(corner[3], lo, hi)), w11[:, lo:hi], MULT)
+                nc.vector.tensor_tensor(fourth[:, lo:hi], y[b][:].indirect(entries(corner[3], lo, hi)), spread[3][:, lo:hi], MULT)
             for lo, hi in parts:
                 nc.vector.tensor_tensor(result[:, lo:hi], fourth[:, lo:hi], acc[:, lo:hi], ADD)
                 nc.sync.dma_start(out[b * P : (b + 1) * P, lo:hi], result[:, lo:hi])

@@ -22,7 +22,7 @@ PIECE = 256
 PAIR_CHUNKS = (
     ((1024, 0), (512, 512), (512, 192)),
     ((1024, 1024), (512, 0), (512, 192)),
-    ((768, 768), (768, 768), (512, 256)),
+    ((768, 768), (768, 768), (512, 128)),
     ((768, 768), (512, 512), (512, 0), (256, 128)),
 )
 
@@ -90,13 +90,13 @@ def tile_picked_bilin_none_e_kernel(
         )
         spread_ps = []
         for i in range(4):
-            bank = psum.tile([P, V], F32, name=f"spread_ps{i}", tag=("bank0", "bank1", "bank6", "bank7")[i])
+            bank = psum.tile([P, V], F32, name=f"spread_ps{i}", tag=f"bank{4 + i}")
             spread_ps.append(bank)
             for c in range(4):
                 column = weight[:, 4 * i + c : 4 * i + c + 1]
                 nc.tensor.transpose(bank[:, c * P : (c + 1) * P], column.to_broadcast([P, P]), ident[:])
 
-        late1, late2, late3 = 1024, 256, 768
+        late1, late2, late3 = 1024, 384, 0
         first = keep.tile([P, 2 * (2 * T - late1)], BF16, name="first", align_bytes=64)
         second = keep.tile([P, 2 * (2 * T - late3 - late2 + 2 * S)], BF16, name="second", align_bytes=64)
         pairs = [
@@ -121,9 +121,8 @@ def tile_picked_bilin_none_e_kernel(
         grouped0 = second[:, 2 * (2 * T - late3 - late2) :]
         for u in range(2):
             nc.vector.tensor_copy(grouped0.bitcast(U32)[:, u : 2 * S : 2], cast_pair(u).indirect(picked[:]))
-        upper = keep.tile([P, 2, V], F32, name="upper", tag="raw1_2")
-        for i in range(2):
-            nc.scalar.activation(upper[:, i, :], spread_ps[i][:], COPY)
+        w00 = keep.tile([P, V], F32, name="w00", tag="raw1_2")
+        nc.scalar.activation(w00[:], spread_ps[0][:], COPY)
         codes0 = keep.tile([P, S], U32, name="codes0", align_bytes=64)
         scale0 = keep.tile([P, S], U8, name="scale0", align_bytes=64)
         nc.vector.quantize_mx(out=codes0[:].bitcast(FP8X4), scales=scale0[:], in_=grouped0)
@@ -146,13 +145,11 @@ def tile_picked_bilin_none_e_kernel(
             )
 
         banks0 = [psum.tile([P, 512], F32, name=f"y0_ps{i}", tag=f"bank{i}") for i in pieces]
-        banks1 = [psum.tile([P, 512], F32, name=f"y1_ps{h}", tag=f"bank{4 + h}") for h in range(2)]
+        early = psum.tile([P, 512], F32, name="y1_ps0", tag="bank4")
         for i in pieces:
             cols = slice(i * PIECE, (i + 1) * PIECE)
             product(banks0[i][:, 0:PIECE], 0, 0, codes0[:, cols], scale0[:, cols])
-        for h in range(2):
-            cols = slice(h * 512, (h + 1) * 512)
-            product(banks1[h][:], 1, 0, codes0[:, cols], scale0[:, cols])
+        product(early[:], 1, 0, codes0[:, 0:512], scale0[:, 0:512])
         y = [keep.tile([P, S], F32, name=f"y{b}") for b in range(2)]
         made = []
         for h in range(2):
@@ -170,19 +167,23 @@ def tile_picked_bilin_none_e_kernel(
             for j in range(2):
                 cols = slice(j * PIECE, (j + 1) * PIECE)
                 product(banks0[2 * h + j][:, 0:PIECE], 0, 1, codes1[:, cols], scale1[:, cols])
-        for h in range(2):
-            product(banks1[h][:], 1, 1, made[h][0][:], made[h][1][:])
+        product(early[:], 1, 1, made[0][0][:], made[0][1][:])
         for i in pieces:
             if i == len(pieces) - 1:
                 nc.vector.tensor_copy(y[0][:, i * PIECE : (i + 1) * PIECE], banks0[i][:, 0:PIECE])
             else:
                 nc.scalar.activation(y[0][:, i * PIECE : (i + 1) * PIECE], banks0[i][:, 0:PIECE], COPY)
+        late = psum.tile([P, 512], F32, name="y1_ps1", tag="bank3")
+        product(late[:], 1, 0, codes0[:, 512:1024], scale0[:, 512:1024])
+        product(late[:], 1, 1, made[1][0][:], made[1][1][:])
+        w01 = keep.tile([P, V], F32, name="w01", tag="codes1_0", align_bytes=64)
+        nc.scalar.activation(w01[:], spread_ps[1][:], COPY)
         lower = keep.tile([P, 2, V], F32, name="lower", tag="codes1_1", align_bytes=64)
         nc.scalar.activation(lower[:, 0, :], spread_ps[2][:], COPY)
-        for h in range(2):
-            nc.scalar.activation(y[1][:, h * 512 : (h + 1) * 512], banks1[h][:], COPY)
+        for h, bank in enumerate((early, late)):
+            nc.scalar.activation(y[1][:, h * 512 : (h + 1) * 512], bank[:], COPY)
         nc.scalar.activation(lower[:, 1, :], spread_ps[3][:], COPY)
-        spread = [upper[:, 0, :], upper[:, 1, :], lower[:, 0, :], lower[:, 1, :]]
+        spread = [w00[:], w01[:], lower[:, 0, :], lower[:, 1, :]]
 
         accs = []
         for b in range(2):
@@ -202,17 +203,23 @@ def tile_picked_bilin_none_e_kernel(
             three = keep.tile([P, V], F32, name=f"three{b}")
             for h in range(2):
                 nc.scalar.activation(three[:, h * 256 : (h + 1) * 256], turned[:, h * 256 : (h + 1) * 256], COPY)
-            acc = psum.tile([P, V], F32, name=f"acc{b}", tag=f"bank{2 + b}")
+            acc = psum.tile([P, V], F32, name=f"acc{b}", tag=f"bank{2 + 3 * b}")
             accs.append(acc)
             for c in range(4):
                 nc.tensor.transpose(acc[:, c * P : (c + 1) * P], three[:, c * P : (c + 1) * P], ident[:])
-        for b in range(2):
-            acc = accs[b]
-            fourth = keep.tile([P, V], F32, name=f"fourth{b}", tag="got0_1")
-            result = keep.tile([P, V], F32, name=f"result{b}")
-            parts = ((0, V),) if b == 0 else ((0, V // 2), (V // 2, V))
-            for lo, hi in parts:
-                nc.vector.tensor_tensor(fourth[:, lo:hi], y[b][:].indirect(entries(corner[3], lo, hi)), spread[3][:, lo:hi], MULT)
-            for lo, hi in parts:
-                nc.vector.tensor_tensor(result[:, lo:hi], fourth[:, lo:hi], acc[:, lo:hi], ADD)
-                nc.sync.dma_start(out[b * P : (b + 1) * P, lo:hi], result[:, lo:hi])
+        fourth = [keep.tile([P, V], F32, name="fourth0", tag="got0_1"), keep.tile([P, V], F32, name="fourth1")]
+        result = [keep.tile([P, V], F32, name=f"result{b}") for b in range(2)]
+
+        def fetch(b, lo, hi):
+            nc.vector.tensor_tensor(fourth[b][:, lo:hi], y[b][:].indirect(entries(corner[3], lo, hi)), spread[3][:, lo:hi], MULT)
+
+        def finish(b, lo, hi):
+            nc.vector.tensor_tensor(result[b][:, lo:hi], fourth[b][:, lo:hi], accs[b][:, lo:hi], ADD)
+            nc.sync.dma_start(out[b * P : (b + 1) * P, lo:hi], result[b][:, lo:hi])
+
+        parts = [(b, lo, lo + V // 2) for b in range(2) for lo in (0, V // 2)]
+        fetch(*parts[0])
+        for ahead, behind in zip(parts[1:], parts):
+            fetch(*ahead)
+            finish(*behind)
+        finish(*parts[-1])

@@ -21,9 +21,9 @@ ADD = mybir.AluOpType.add
 PIECE = 256
 PAIR_CHUNKS = (
     ((1024, 0), (512, 512), (512, 192)),
-    ((1024, 1024), (512, 0), (512, 192)),
-    ((768, 768), (768, 768), (512, 128)),
-    ((768, 768), (512, 512), (512, 0), (256, 128)),
+    ((512, 512), (512, 512), (512, 512), (512, 192)),
+    ((512, 512), (512, 512), (512, 512), (512, 320)),
+    ((512, 512), (512, 512), (512, 320), (384, 128), (128, 128)),
 )
 
 
@@ -96,15 +96,12 @@ def tile_picked_bilin_none_e_kernel(
                 column = weight[:, 4 * i + c : 4 * i + c + 1]
                 nc.tensor.transpose(bank[:, c * P : (c + 1) * P], column.to_broadcast([P, P]), ident[:])
 
-        late1, late2, late3 = 1024, 384, 0
-        first = keep.tile([P, 2 * (2 * T - late1)], BF16, name="first", align_bytes=64)
-        second = keep.tile([P, 2 * (2 * T - late3 - late2 + 2 * S)], BF16, name="second", align_bytes=64)
-        pairs = [
-            first[:, 2 * (T - late1) : 2 * (2 * T - late1)],
-            first[:, 0 : 2 * T],
-            second[:, 2 * (T - late3) : 2 * (2 * T - late3)],
-            second[:, 0 : 2 * T],
-        ]
+        late = 320
+        first = keep.tile([P, 2 * (2 * T - late)], BF16, name="first")
+        pairs = [first[:, 2 * (T - late) : 2 * (2 * T - late)], first[:, 0 : 2 * T]]
+        second = keep.tile([P, 2 * (T - 192 + S)], BF16, name="second", align_bytes=64)
+        pairs.append(second[:, 0 : 2 * T])
+        pairs.append(keep.tile([P, 2 * T], BF16, name="pair3")[:])
 
         def cast_pair(i):
             pair = pairs[i]
@@ -118,14 +115,20 @@ def tile_picked_bilin_none_e_kernel(
             return pair.bitcast(U32)
 
         pieces = range(S // PIECE)
-        grouped0 = second[:, 2 * (2 * T - late3 - late2) :]
+        grouped0 = [second[:, 2 * (T - 192) :], keep.tile([P, 2 * S], BF16, name="grouped0_1", align_bytes=64)[:]]
         for u in range(2):
-            nc.vector.tensor_copy(grouped0.bitcast(U32)[:, u : 2 * S : 2], cast_pair(u).indirect(picked[:]))
-        w00 = keep.tile([P, V], F32, name="w00", tag="raw1_2")
+            window = cast_pair(u)
+            for h in range(2):
+                nc.vector.tensor_copy(
+                    grouped0[h].bitcast(U32)[:, u:S:2], window.indirect(entries(picked, 512 * h, 512 * (h + 1)))
+                )
+        w00 = keep.tile([P, V], F32, name="w00", tag="raw1_3")
         nc.scalar.activation(w00[:], spread_ps[0][:], COPY)
         codes0 = keep.tile([P, S], U32, name="codes0", align_bytes=64)
         scale0 = keep.tile([P, S], U8, name="scale0", align_bytes=64)
-        nc.vector.quantize_mx(out=codes0[:].bitcast(FP8X4), scales=scale0[:], in_=grouped0)
+        for h in range(2):
+            cols = slice(512 * h, 512 * (h + 1))
+            nc.vector.quantize_mx(out=codes0[:, cols].bitcast(FP8X4), scales=scale0[:, cols], in_=grouped0[h])
 
         halves1 = [keep.tile([P, 2, PIECE], U32, name=f"halves1_{i}") for i in pieces]
         for u in range(2):
@@ -169,18 +172,15 @@ def tile_picked_bilin_none_e_kernel(
                 product(banks0[2 * h + j][:, 0:PIECE], 0, 1, codes1[:, cols], scale1[:, cols])
         product(early[:], 1, 1, made[0][0][:], made[0][1][:])
         for i in pieces:
-            if i == len(pieces) - 1:
-                nc.vector.tensor_copy(y[0][:, i * PIECE : (i + 1) * PIECE], banks0[i][:, 0:PIECE])
-            else:
-                nc.scalar.activation(y[0][:, i * PIECE : (i + 1) * PIECE], banks0[i][:, 0:PIECE], COPY)
-        late = psum.tile([P, 512], F32, name="y1_ps1", tag="bank3")
-        product(late[:], 1, 0, codes0[:, 512:1024], scale0[:, 512:1024])
-        product(late[:], 1, 1, made[1][0][:], made[1][1][:])
-        w01 = keep.tile([P, V], F32, name="w01", tag="codes1_0", align_bytes=64)
-        nc.scalar.activation(w01[:], spread_ps[1][:], COPY)
+            nc.scalar.activation(y[0][:, i * PIECE : (i + 1) * PIECE], banks0[i][:, 0:PIECE], COPY)
+        behind = psum.tile([P, 512], F32, name="y1_ps1", tag="bank3")
+        product(behind[:], 1, 0, codes0[:, 512:1024], scale0[:, 512:1024])
+        product(behind[:], 1, 1, made[1][0][:], made[1][1][:])
+        w01 = keep.tile([P, V], F32, name="w01", tag="grouped1_3", align_bytes=64)
+        nc.vector.tensor_copy(w01[:], spread_ps[1][:])
         lower = keep.tile([P, 2, V], F32, name="lower", tag="codes1_1", align_bytes=64)
         nc.scalar.activation(lower[:, 0, :], spread_ps[2][:], COPY)
-        for h, bank in enumerate((early, late)):
+        for h, bank in enumerate((early, behind)):
             nc.scalar.activation(y[1][:, h * 512 : (h + 1) * 512], bank[:], COPY)
         nc.scalar.activation(lower[:, 1, :], spread_ps[3][:], COPY)
         spread = [w00[:], w01[:], lower[:, 0, :], lower[:, 1, :]]

@@ -20,10 +20,10 @@ ADD = mybir.AluOpType.add
 
 PIECE = 256
 PAIR_CHUNKS = (
-    ((1024, 0), (512, 512), (512, 192)),
-    ((512, 512), (512, 512), (512, 512), (512, 192)),
-    ((512, 512), (512, 512), (512, 512), (512, 320)),
-    ((512, 512), (512, 512), (512, 320), (384, 128), (128, 128)),
+    ((0, 1024, 512), (1024, 1024, 400)),
+    ((0, 1024, 1024), (1024, 1024, 400)),
+    ((0, 1024, 1024), (1024, 1024, 400)),
+    ((0, 512, 512), (512, 512, 512), (1024, 512, 512), (1664, 384, 0), (1536, 128, 128)),
 )
 
 
@@ -42,25 +42,23 @@ def tile_picked_bilin_none_e_kernel(
             return lst[:, lo // 16 : hi // 16]
 
         ident = keep.tile([P, P], F32, name="ident")
-        frac_rows = keep.tile([P, P], F32, name="frac_rows")
         w_scale = keep.tile([P, N], U8, name="w_scale", align_bytes=64)
-        nc.gpsimd.memset(frac_rows[:], 0.0)
         nc.gpsimd.memset(w_scale[:].bitcast(I32), 0)
         make_identity(nc, ident[:])
 
         picked = keep.tile([P, S // 16], U16, name="picked")
+        sides = keep.tile([P, 2, 2, 4], F32, name="sides")
+        for axis, frac in enumerate((fx, fy)):
+            nc.scalar.dma_start(sides[:, axis, 1, :], frac[0:1, :].rearrange("o (p c) -> (o p) c", c=4))
         raw = []
         for i in range(4):
-            chunks, lo = [], 0
-            for j, (width, cut) in enumerate(PAIR_CHUNKS[i]):
-                chunk = keep.tile([P, 2, width], F32, name=f"raw{i}_{j}")
+            chunks = []
+            for j, (lo, width, cut) in enumerate(PAIR_CHUNKS[i]):
+                chunk = keep.tile([P, 2, width], F32, name=f"raw{i}_{j}", align_bytes=64)
                 nc.sync.dma_start(chunk[:], rows(i // 2)[:, 2 * (i % 2) : 2 * (i % 2) + 2, lo : lo + width])
                 chunks.append((chunk, lo, width, cut))
-                lo = lo + width
                 if (i, j) == (0, 0):
                     nc.sync.dma_start(picked[:], offs)
-                    nc.sync.dma_start(frac_rows[0:4, :], fx[0:1, :].rearrange("o (c p) -> (o c) p", p=P))
-                    nc.sync.dma_start(frac_rows[4:8, :], fy[0:1, :].rearrange("o (c p) -> (o c) p", p=P))
             raw.append(chunks)
         w_words = [keep.tile([P, N], U32, name=f"w_words{z}", align_bytes=64) for z in range(2)]
         for z in range(2):
@@ -76,16 +74,12 @@ def tile_picked_bilin_none_e_kernel(
             nc.sync.dma_start(tile[:], lst)
             corner.append(tile)
 
-        frac_ps = psum.tile([P, 512], F32, name="frac_ps", tag="bank2")
-        nc.tensor.transpose(frac_ps[:, 0:P], frac_rows[:], ident[:])
-        sides = keep.tile([P, 2, 8], F32, name="sides")
-        nc.vector.tensor_scalar(sides[:, 0, :], frac_ps[:, 0:8], -1.0, 1.0, MULT, ADD)
-        nc.vector.tensor_copy(sides[:, 1, :], frac_ps[:, 0:8])
+        nc.gpsimd.tensor_scalar(sides[:, :, 0, :], sides[:, :, 1, :], -1.0, 1.0, MULT, ADD)
         weight = keep.tile([P, 16], F32, name="weight")
         nc.gpsimd.tensor_tensor(
             weight[:].rearrange("p (j i c) -> p j i c", j=2, i=2),
-            sides[:, :, 0:4].unsqueeze(1).to_broadcast([P, 2, 2, 4]),
-            sides[:, :, 4:8].unsqueeze(2).to_broadcast([P, 2, 2, 4]),
+            sides[:, 0, :, :].unsqueeze(1).to_broadcast([P, 2, 2, 4]),
+            sides[:, 1, :, :].unsqueeze(2).to_broadcast([P, 2, 2, 4]),
             MULT,
         )
         spread_ps = []
@@ -96,12 +90,15 @@ def tile_picked_bilin_none_e_kernel(
                 column = weight[:, 4 * i + c : 4 * i + c + 1]
                 nc.tensor.transpose(bank[:, c * P : (c + 1) * P], column.to_broadcast([P, P]), ident[:])
 
-        late = 320
+        late, last = 624, 384
         first = keep.tile([P, 2 * (2 * T - late)], BF16, name="first")
         pairs = [first[:, 2 * (T - late) : 2 * (2 * T - late)], first[:, 0 : 2 * T]]
-        second = keep.tile([P, 2 * (T - 192 + S)], BF16, name="second", align_bytes=64)
+        second = keep.tile([P, 2 * (2 * T - last - late + S)], BF16, name="second", align_bytes=64)
+        pairs.append(second[:, 2 * (T - last) : 2 * (2 * T - last)])
         pairs.append(second[:, 0 : 2 * T])
-        pairs.append(keep.tile([P, 2 * T], BF16, name="pair3")[:])
+
+        def in_order(dst, bank):
+            return dst.rearrange("p (n c) -> p n c", c=4), bank.rearrange("p (c n) -> p n c", c=4)
 
         def cast_pair(i):
             pair = pairs[i]
@@ -115,21 +112,23 @@ def tile_picked_bilin_none_e_kernel(
             return pair.bitcast(U32)
 
         pieces = range(S // PIECE)
-        grouped0 = [second[:, 2 * (T - 192) :], keep.tile([P, 2 * S], BF16, name="grouped0_1", align_bytes=64)[:]]
+        grouped0 = [second[:, 2 * (2 * T - last - late) :], keep.tile([P, 2 * S], BF16, name="grouped0_1", align_bytes=64)[:]]
         for u in range(2):
             window = cast_pair(u)
             for h in range(2):
                 nc.vector.tensor_copy(
                     grouped0[h].bitcast(U32)[:, u:S:2], window.indirect(entries(picked, 512 * h, 512 * (h + 1)))
                 )
-        w00 = keep.tile([P, V], F32, name="w00", tag="raw1_3")
-        nc.scalar.activation(w00[:], spread_ps[0][:], COPY)
+        spread = []
+        for i in range(4):
+            wide = keep.tile([P, V], F32, name=f"w{i}", tag=f"raw{i // 2}_{1 - i % 2}", align_bytes=64)
+            nc.scalar.activation(*in_order(wide[:], spread_ps[i][:]), COPY)
+            spread.append(wide[:])
         codes0 = keep.tile([P, S], U32, name="codes0", align_bytes=64)
         scale0 = keep.tile([P, S], U8, name="scale0", align_bytes=64)
         for h in range(2):
             cols = slice(512 * h, 512 * (h + 1))
             nc.vector.quantize_mx(out=codes0[:, cols].bitcast(FP8X4), scales=scale0[:, cols], in_=grouped0[h])
-
         halves1 = [keep.tile([P, 2, PIECE], U32, name=f"halves1_{i}") for i in pieces]
         for u in range(2):
             window = cast_pair(2 + u)
@@ -176,14 +175,8 @@ def tile_picked_bilin_none_e_kernel(
         behind = psum.tile([P, 512], F32, name="y1_ps1", tag="bank3")
         product(behind[:], 1, 0, codes0[:, 512:1024], scale0[:, 512:1024])
         product(behind[:], 1, 1, made[1][0][:], made[1][1][:])
-        w01 = keep.tile([P, V], F32, name="w01", tag="grouped1_3", align_bytes=64)
-        nc.vector.tensor_copy(w01[:], spread_ps[1][:])
-        lower = keep.tile([P, 2, V], F32, name="lower", tag="codes1_1", align_bytes=64)
-        nc.scalar.activation(lower[:, 0, :], spread_ps[2][:], COPY)
         for h, bank in enumerate((early, behind)):
             nc.scalar.activation(y[1][:, h * 512 : (h + 1) * 512], bank[:], COPY)
-        nc.scalar.activation(lower[:, 1, :], spread_ps[3][:], COPY)
-        spread = [w00[:], w01[:], lower[:, 0, :], lower[:, 1, :]]
 
         accs = []
         for b in range(2):

@@ -20,9 +20,9 @@ ADD = mybir.AluOpType.add
 
 PIECE = 256
 PAIR_CHUNKS = (
-    ((0, 1024, 512), (1024, 1024, 400)),
-    ((0, 1024, 1024), (1024, 1024, 400)),
-    ((0, 1024, 1024), (1024, 1024, 400)),
+    ((0, 1024, 0), (1024, 1024, 400)),
+    ((0, 768, 768), (768, 768, 768), (1536, 512, 128)),
+    ((0, 768, 768), (768, 768, 768), (1536, 512, 128)),
     ((0, 512, 512), (512, 512, 512), (1024, 512, 512), (1664, 384, 0), (1536, 128, 128)),
 )
 
@@ -90,7 +90,7 @@ def tile_picked_bilin_none_e_kernel(
                 column = weight[:, 4 * i + c : 4 * i + c + 1]
                 nc.tensor.transpose(bank[:, c * P : (c + 1) * P], column.to_broadcast([P, P]), ident[:])
 
-        late, last = 624, 384
+        late, last = 384, 384
         first = keep.tile([P, 2 * (2 * T - late)], BF16, name="first")
         pairs = [first[:, 2 * (T - late) : 2 * (2 * T - late)], first[:, 0 : 2 * T]]
         second = keep.tile([P, 2 * (2 * T - last - late + S)], BF16, name="second", align_bytes=64)
@@ -119,11 +119,8 @@ def tile_picked_bilin_none_e_kernel(
                 nc.vector.tensor_copy(
                     grouped0[h].bitcast(U32)[:, u:S:2], window.indirect(entries(picked, 512 * h, 512 * (h + 1)))
                 )
-        spread = []
-        for i in range(4):
-            wide = keep.tile([P, V], F32, name=f"w{i}", tag=f"raw{i // 2}_{1 - i % 2}", align_bytes=64)
-            nc.scalar.activation(*in_order(wide[:], spread_ps[i][:]), COPY)
-            spread.append(wide[:])
+        w00 = keep.tile([P, V], F32, name="w00", tag="raw1_2", align_bytes=64)
+        nc.scalar.activation(*in_order(w00[:], spread_ps[0][:]), COPY)
         codes0 = keep.tile([P, S], U32, name="codes0", align_bytes=64)
         scale0 = keep.tile([P, S], U8, name="scale0", align_bytes=64)
         for h in range(2):
@@ -175,8 +172,14 @@ def tile_picked_bilin_none_e_kernel(
         behind = psum.tile([P, 512], F32, name="y1_ps1", tag="bank3")
         product(behind[:], 1, 0, codes0[:, 512:1024], scale0[:, 512:1024])
         product(behind[:], 1, 1, made[1][0][:], made[1][1][:])
+        w01 = keep.tile([P, V], F32, name="w01", tag="grouped1_3", align_bytes=64)
+        nc.vector.tensor_copy(*in_order(w01[:], spread_ps[1][:]))
+        lower = keep.tile([P, 2, V], F32, name="lower", tag="codes1_1", align_bytes=64)
+        nc.scalar.activation(*in_order(lower[:, 0, :], spread_ps[2][:]), COPY)
         for h, bank in enumerate((early, behind)):
             nc.scalar.activation(y[1][:, h * 512 : (h + 1) * 512], bank[:], COPY)
+        nc.scalar.activation(*in_order(lower[:, 1, :], spread_ps[3][:]), COPY)
+        spread = [w00[:], w01[:], lower[:, 0, :], lower[:, 1, :]]
 
         accs = []
         for b in range(2):

@@ -19,12 +19,7 @@ MULT = mybir.AluOpType.mult
 ADD = mybir.AluOpType.add
 
 PIECE = 256
-PAIR_CHUNKS = (
-    ((0, 1024, 0), (1024, 1024, 400)),
-    ((0, 768, 768), (768, 768, 768), (1536, 512, 128)),
-    ((0, 768, 768), (768, 768, 768), (1536, 512, 128)),
-    ((0, 512, 512), (512, 512, 512), (1024, 512, 512), (1664, 384, 0), (1536, 128, 128)),
-)
+PIECES = S // PIECE
 
 
 def tile_picked_bilin_none_e_kernel(
@@ -34,9 +29,6 @@ def tile_picked_bilin_none_e_kernel(
     with ExitStack() as ctx:
         keep = ctx.enter_context(tc.tile_pool(name="keep", bufs=1))
         psum = ctx.enter_context(tc.psum_pool(name="psum", bufs=1))
-
-        def rows(z):
-            return xT[512 * z : 512 * (z + 1), :].rearrange("(p j) t -> p j t", j=4)
 
         def entries(lst, lo, hi):
             return lst[:, lo // 16 : hi // 16]
@@ -50,24 +42,23 @@ def tile_picked_bilin_none_e_kernel(
         sides = keep.tile([P, 2, 2, 4], F32, name="sides")
         for axis, frac in enumerate((fx, fy)):
             nc.scalar.dma_start(sides[:, axis, 1, :], frac[0:1, :].rearrange("o (p c) -> (o p) c", c=4))
-        raw = []
-        for i in range(4):
-            chunks = []
-            for j, (lo, width, cut) in enumerate(PAIR_CHUNKS[i]):
-                chunk = keep.tile([P, 2, width], F32, name=f"raw{i}_{j}", align_bytes=64)
-                nc.sync.dma_start(chunk[:], rows(i // 2)[:, 2 * (i % 2) : 2 * (i % 2) + 2, lo : lo + width])
-                chunks.append((chunk, lo, width, cut))
-                if (i, j) == (0, 0):
+        planes = []
+        for z in range(2):
+            rows = xT[512 * z : 512 * (z + 1), :].rearrange("(p t) c -> p t c", t=4)
+            for t in range(4):
+                plane = keep.tile([P, T], F32, name=f"plane{z}_{t}")
+                nc.sync.dma_start(plane[:], rows[:, t, :])
+                planes.append(plane)
+                if (z, t) == (0, 0):
                     nc.sync.dma_start(picked[:], offs)
-            raw.append(chunks)
+                if (z, t) == (0, 2):
+                    for q in range(4):
+                        nc.sync.dma_start(
+                            w_scale[32 * q : 32 * q + 8, :].bitcast(I32), w1_scales[:, 4 * q : 4 * q + 4, :].bitcast(I32)
+                        )
         w_words = [keep.tile([P, N], U32, name=f"w_words{z}", align_bytes=64) for z in range(2)]
         for z in range(2):
             nc.sync.dma_start(w_words[z][:].bitcast(I32), w1_words[z].rearrange("p n t -> p (n t)").bitcast(I32))
-            if z == 0:
-                for q in range(4):
-                    nc.sync.dma_start(
-                        w_scale[32 * q : 32 * q + 8, :].bitcast(I32), w1_scales[:, 4 * q : 4 * q + 4, :].bitcast(I32)
-                    )
         corner = []
         for i, lst in enumerate((c00, c01, c10, c11)):
             tile = keep.tile([P, V // 16], U16, name=f"corner{i}")
@@ -89,133 +80,143 @@ def tile_picked_bilin_none_e_kernel(
             for c in range(4):
                 column = weight[:, 4 * i + c : 4 * i + c + 1]
                 nc.tensor.transpose(bank[:, c * P : (c + 1) * P], column.to_broadcast([P, P]), ident[:])
+        spread = [keep.tile([P, V], F32, name=f"spread{i}") for i in range(4)]
 
-        late, last = 384, 384
-        first = keep.tile([P, 2 * (2 * T - late)], BF16, name="first")
-        pairs = [first[:, 2 * (T - late) : 2 * (2 * T - late)], first[:, 0 : 2 * T]]
-        second = keep.tile([P, 2 * (2 * T - last - late + S)], BF16, name="second", align_bytes=64)
-        pairs.append(second[:, 2 * (T - last) : 2 * (2 * T - last)])
-        pairs.append(second[:, 0 : 2 * T])
+        def unload_weight(i):
+            nc.vector.tensor_copy(
+                spread[i][:].rearrange("p (n c) -> p n c", c=4), spread_ps[i][:].rearrange("p (c n) -> p n c", c=4)
+            )
 
-        def in_order(dst, bank):
-            return dst.rearrange("p (n c) -> p n c", c=4), bank.rearrange("p (c n) -> p n c", c=4)
+        woven = [[keep.tile([P, PIECE, 4], BF16, name=f"woven{z}_{i}", align_bytes=64) for i in range(PIECES)] for z in range(2)]
+        codes = [[keep.tile([P, PIECE], U32, name=f"codes{z}_{i}", align_bytes=64) for i in range(PIECES)] for z in range(2)]
+        scale = [[keep.tile([P, PIECE], U8, name=f"scale{z}_{i}", align_bytes=64) for i in range(PIECES)] for z in range(2)]
+        flat = {}
 
-        def cast_pair(i):
-            pair = pairs[i]
-            for chunk, lo, width, cut in raw[i]:
-                src = chunk[:].rearrange("p u c -> p c u")
-                dst = pair[:, 2 * lo : 2 * (lo + width)].rearrange("p (c u) -> p c u", u=2)
-                if cut > 0:
-                    nc.scalar.activation(dst[:, 0:cut, :], src[:, 0:cut, :], COPY)
-                if cut < width:
-                    nc.vector.tensor_copy(dst[:, cut:width, :], src[:, cut:width, :])
-            return pair.bitcast(U32)
+        def gather(z, t, i):
+            window = planes[4 * z + t][:].indirect(entries(picked, i * PIECE, (i + 1) * PIECE))
+            if i == 0:
+                nc.vector.tensor_copy(woven[z][0][:, :, t], window)
+            else:
+                if t % 2 == 0:
+                    flat[z, t // 2, i] = keep.tile([P, 2, PIECE], BF16, name=f"flat{z}_{t // 2}_{i}")
+                nc.scalar.activation(flat[z, t // 2, i][:, t % 2, :], window, COPY)
 
-        pieces = range(S // PIECE)
-        grouped0 = [second[:, 2 * (2 * T - last - late) :], keep.tile([P, 2 * S], BF16, name="grouped0_1", align_bytes=64)[:]]
-        for u in range(2):
-            window = cast_pair(u)
-            for h in range(2):
-                nc.vector.tensor_copy(
-                    grouped0[h].bitcast(U32)[:, u:S:2], window.indirect(entries(picked, 512 * h, 512 * (h + 1)))
-                )
-        w00 = keep.tile([P, V], F32, name="w00", tag="raw1_2", align_bytes=64)
-        nc.scalar.activation(*in_order(w00[:], spread_ps[0][:]), COPY)
-        codes0 = keep.tile([P, S], U32, name="codes0", align_bytes=64)
-        scale0 = keep.tile([P, S], U8, name="scale0", align_bytes=64)
-        for h in range(2):
-            cols = slice(512 * h, 512 * (h + 1))
-            nc.vector.quantize_mx(out=codes0[:, cols].bitcast(FP8X4), scales=scale0[:, cols], in_=grouped0[h])
-        halves1 = [keep.tile([P, 2, PIECE], U32, name=f"halves1_{i}") for i in pieces]
-        for u in range(2):
-            window = cast_pair(2 + u)
-            for i in pieces:
-                nc.vector.tensor_copy(halves1[i][:, u, :], window.indirect(entries(picked, i * PIECE, (i + 1) * PIECE)))
+        def place(z, u, i, on_scalar=False):
+            dst = woven[z][i][:, :, 2 * u : 2 * u + 2]
+            src = flat[z, u, i][:].rearrange("p u n -> p n u")
+            if on_scalar:
+                nc.scalar.activation(dst, src, COPY)
+            else:
+                nc.vector.tensor_copy(dst, src)
 
-        def product(bank, b, z, codes, scale):
+        def quantise(z, i):
+            nc.vector.quantize_mx(
+                out=codes[z][i][:].bitcast(FP8X4), scales=scale[z][i][:], in_=woven[z][i][:].rearrange("p n t -> p (n t)")
+            )
+
+        def product(bank, b, z, i):
             nc.tensor.matmul_mx(
                 out=bank,
                 lhsT=w_words[z][:, b * P : (b + 1) * P].bitcast(FP8X4),
                 lhsT_scale=w_scale[4 * z : P, b * P : (b + 1) * P],
-                rhs=codes.bitcast(FP8X4),
-                rhs_scale=scale,
+                rhs=codes[z][i][:].bitcast(FP8X4),
+                rhs_scale=scale[z][i][:],
                 start=(z == 0),
                 stop=(z == 1),
             )
 
-        banks0 = [psum.tile([P, 512], F32, name=f"y0_ps{i}", tag=f"bank{i}") for i in pieces]
-        early = psum.tile([P, 512], F32, name="y1_ps0", tag="bank4")
-        for i in pieces:
-            cols = slice(i * PIECE, (i + 1) * PIECE)
-            product(banks0[i][:, 0:PIECE], 0, 0, codes0[:, cols], scale0[:, cols])
-        product(early[:], 1, 0, codes0[:, 0:512], scale0[:, 0:512])
+        for z in range(2):
+            for t in range(4):
+                for i in range(PIECES):
+                    gather(z, t, i)
+                if z == 0:
+                    unload_weight(t)
+                if t % 2 == 1 and (z, t) != (1, 3):
+                    for i in range(1, PIECES):
+                        place(z, t // 2, i)
+            if z == 0:
+                for i in range(PIECES):
+                    quantise(0, i)
+        banks = [[psum.tile([P, 512], F32, name=f"y_ps{b}_{i}", tag=f"bank{4 * b + i}") for i in range(PIECES)] for b in range(2)]
+        for i in range(PIECES):
+            product(banks[0][i][:, 0:PIECE], 0, 0, i)
+        place(1, 1, 1)
+        quantise(1, 0)
+        place(1, 1, 2)
+        quantise(1, 1)
+        place(1, 1, 3, on_scalar=True)
+        quantise(1, 2)
+        quantise(1, 3)
         y = [keep.tile([P, S], F32, name=f"y{b}") for b in range(2)]
-        made = []
-        for h in range(2):
-            codes1 = keep.tile([P, 512], U32, name=f"codes1_{h}", align_bytes=64)
-            scale1 = keep.tile([P, 512], U8, name=f"scale1_{h}", align_bytes=64)
-            made.append((codes1, scale1))
-            for j in range(2):
-                i = 2 * h + j
-                cols = slice(j * PIECE, (j + 1) * PIECE)
-                grouped1 = keep.tile([P, 4 * PIECE], BF16, name=f"grouped1_{i}", align_bytes=64)
-                nc.scalar.copy(
-                    grouped1[:].bitcast(U32).rearrange("p (n u) -> p n u", u=2), halves1[i][:].rearrange("p u n -> p n u")
-                )
-                nc.vector.quantize_mx(out=codes1[:, cols].bitcast(FP8X4), scales=scale1[:, cols], in_=grouped1[:])
-            for j in range(2):
-                cols = slice(j * PIECE, (j + 1) * PIECE)
-                product(banks0[2 * h + j][:, 0:PIECE], 0, 1, codes1[:, cols], scale1[:, cols])
-        product(early[:], 1, 1, made[0][0][:], made[0][1][:])
-        for i in pieces:
-            nc.scalar.activation(y[0][:, i * PIECE : (i + 1) * PIECE], banks0[i][:, 0:PIECE], COPY)
-        behind = psum.tile([P, 512], F32, name="y1_ps1", tag="bank3")
-        product(behind[:], 1, 0, codes0[:, 512:1024], scale0[:, 512:1024])
-        product(behind[:], 1, 1, made[1][0][:], made[1][1][:])
-        w01 = keep.tile([P, V], F32, name="w01", tag="grouped1_3", align_bytes=64)
-        nc.vector.tensor_copy(*in_order(w01[:], spread_ps[1][:]))
-        lower = keep.tile([P, 2, V], F32, name="lower", tag="codes1_1", align_bytes=64)
-        nc.scalar.activation(*in_order(lower[:, 0, :], spread_ps[2][:]), COPY)
-        for h, bank in enumerate((early, behind)):
-            nc.scalar.activation(y[1][:, h * 512 : (h + 1) * 512], bank[:], COPY)
-        nc.scalar.activation(*in_order(lower[:, 1, :], spread_ps[3][:]), COPY)
-        spread = [w00[:], w01[:], lower[:, 0, :], lower[:, 1, :]]
+        for i in range(PIECES):
+            product(banks[0][i][:, 0:PIECE], 0, 1, i)
+            nc.scalar.activation(y[0][:, i * PIECE : (i + 1) * PIECE], banks[0][i][:, 0:PIECE], COPY)
+        for i in range(PIECES):
+            product(banks[1][i][:, 0:PIECE], 1, 0, i)
+            product(banks[1][i][:, 0:PIECE], 1, 1, i)
+        for i in range(2):
+            nc.vector.tensor_copy(y[1][:, i * PIECE : (i + 1) * PIECE], banks[1][i][:, 0:PIECE])
 
-        accs = []
-        for b in range(2):
-            turned = psum.tile([P, V], F32, name=f"turned{b}", tag=f"bank{b}")
-            for i in range(3):
-                got = keep.tile([P, V], F32, name=f"got{i}_{b}", tag=f"got{i}_{b}")
-                nc.vector.tensor_tensor(got[:], y[b][:].indirect(corner[i][:]), spread[i], MULT)
-                for c in range(4):
-                    nc.tensor.matmul(
-                        turned[:, c * P : (c + 1) * P],
-                        got[:, c * P : (c + 1) * P],
-                        ident[:],
-                        start=(i == 0 and c == 0),
-                        stop=(i == 2 and c == 3),
-                        is_transpose=True,
-                    )
-            three = keep.tile([P, V], F32, name=f"three{b}")
-            for h in range(2):
-                nc.scalar.activation(three[:, h * 256 : (h + 1) * 256], turned[:, h * 256 : (h + 1) * 256], COPY)
-            acc = psum.tile([P, V], F32, name=f"acc{b}", tag=f"bank{2 + 3 * b}")
-            accs.append(acc)
+        def fused(b, i, lo=0, hi=V):
+            nc.vector.tensor_tensor(got[b][i][:, lo:hi], y[b][:].indirect(entries(corner[i], lo, hi)), spread[i][:, lo:hi], MULT)
+
+        def fetch(b, i):
+            nc.scalar.activation(plain[b, i][:], y[b][:].indirect(corner[i][:]), COPY)
+
+        def weigh(b, i):
+            nc.vector.tensor_tensor(got[b][i][:], plain[b, i][:], spread[i][:], MULT)
+
+        def turn(b, i, first, last):
             for c in range(4):
-                nc.tensor.transpose(acc[:, c * P : (c + 1) * P], three[:, c * P : (c + 1) * P], ident[:])
-        fourth = [keep.tile([P, V], F32, name="fourth0", tag="got0_1"), keep.tile([P, V], F32, name="fourth1")]
+                nc.tensor.matmul(
+                    turned[b][:, c * P : (c + 1) * P],
+                    got[b][i][:, c * P : (c + 1) * P],
+                    ident[:],
+                    start=(first and c == 0),
+                    stop=(last and c == 3),
+                    is_transpose=True,
+                )
+
+        def turn_back(b):
+            for h in range(2):
+                nc.scalar.activation(summed[b][:, h * 256 : (h + 1) * 256], turned[b][:, h * 256 : (h + 1) * 256], COPY)
+            for c in range(4):
+                nc.tensor.transpose(acc[b][:, c * P : (c + 1) * P], summed[b][:, c * P : (c + 1) * P], ident[:])
+
+        got = [[keep.tile([P, V], F32, name=f"got{b}_{i}") for i in range(4)] for b in range(2)]
+        plain = {(b, i): keep.tile([P, V], F32, name=f"plain{b}_{i}") for b in range(2) for i in (2, 3)}
+        summed = [keep.tile([P, V], F32, name=f"summed{b}") for b in range(2)]
         result = [keep.tile([P, V], F32, name=f"result{b}") for b in range(2)]
+        turned = [psum.tile([P, V], F32, name=f"turned{b}", tag=f"bank{b}") for b in range(2)]
+        acc = [psum.tile([P, V], F32, name=f"acc{b}", tag=f"bank{2 + b}") for b in range(2)]
 
-        def fetch(b, lo, hi):
-            nc.vector.tensor_tensor(fourth[b][:, lo:hi], y[b][:].indirect(entries(corner[3], lo, hi)), spread[3][:, lo:hi], MULT)
-
-        def finish(b, lo, hi):
-            nc.vector.tensor_tensor(result[b][:, lo:hi], fourth[b][:, lo:hi], accs[b][:, lo:hi], ADD)
-            nc.sync.dma_start(out[b * P : (b + 1) * P, lo:hi], result[b][:, lo:hi])
-
-        parts = [(b, lo, lo + V // 2) for b in range(2) for lo in (0, V // 2)]
-        fetch(*parts[0])
-        for ahead, behind in zip(parts[1:], parts):
-            fetch(*ahead)
-            finish(*behind)
-        finish(*parts[-1])
+        fetch(0, 2)
+        fetch(0, 3)
+        for i in range(2, PIECES):
+            nc.scalar.activation(y[1][:, i * PIECE : (i + 1) * PIECE], banks[1][i][:, 0:PIECE], COPY)
+        fetch(1, 2)
+        fetch(1, 3)
+        fused(0, 0)
+        turn(0, 0, True, False)
+        weigh(0, 2)
+        turn(0, 2, False, False)
+        fused(0, 1)
+        turn(0, 1, False, False)
+        weigh(0, 3)
+        turn(0, 3, False, True)
+        fused(1, 0)
+        turn(1, 0, True, False)
+        weigh(1, 2)
+        turn(1, 2, False, False)
+        weigh(1, 3)
+        turn(1, 3, False, True)
+        turn_back(0)
+        turn_back(1)
+        nc.scalar.activation(result[0][:], acc[0][:], COPY)
+        nc.sync.dma_start(out[0:P, :], result[0][:])
+        for lo in (0, V // 2):
+            fused(1, 1, lo, lo + V // 2)
+        for lo in (0, V // 2):
+            hi = lo + V // 2
+            nc.vector.tensor_tensor(result[1][:, lo:hi], got[1][1][:, lo:hi], acc[1][:, lo:hi], ADD)
+            nc.sync.dma_start(out[P : 2 * P, lo:hi], result[1][:, lo:hi])

@@ -19,7 +19,12 @@ MULT = mybir.AluOpType.mult
 ADD = mybir.AluOpType.add
 
 PIECE = 256
-PIECES = S // PIECE
+HALF = 512
+PARTS = (((0, 512), (512, 1024)), ((0, 256), (256, 512), (512, 768), (768, 896), (896, 1024)))
+FLATS = (
+    (((256, 1024),), ((256, 1024),)),
+    (((256, 1024),), ((256, 512), (512, 768), (768, 1024))),
+)
 
 
 def tile_picked_bilin_none_e_kernel(
@@ -51,11 +56,8 @@ def tile_picked_bilin_none_e_kernel(
                 planes.append(plane)
                 if (z, t) == (0, 0):
                     nc.sync.dma_start(picked[:], offs)
-                if (z, t) == (0, 2):
-                    for q in range(4):
-                        nc.sync.dma_start(
-                            w_scale[32 * q : 32 * q + 8, :].bitcast(I32), w1_scales[:, 4 * q : 4 * q + 4, :].bitcast(I32)
-                        )
+        for q in range(4):
+            nc.sync.dma_start(w_scale[32 * q : 32 * q + 8, :].bitcast(I32), w1_scales[:, 4 * q : 4 * q + 4, :].bitcast(I32))
         w_words = [keep.tile([P, N], U32, name=f"w_words{z}", align_bytes=64) for z in range(2)]
         for z in range(2):
             nc.sync.dma_start(w_words[z][:].bitcast(I32), w1_words[z].rearrange("p n t -> p (n t)").bitcast(I32))
@@ -83,79 +85,129 @@ def tile_picked_bilin_none_e_kernel(
         spread = [keep.tile([P, V], F32, name=f"spread{i}") for i in range(4)]
 
         def unload_weight(i):
-            nc.vector.tensor_copy(
-                spread[i][:].rearrange("p (n c) -> p n c", c=4), spread_ps[i][:].rearrange("p (c n) -> p n c", c=4)
-            )
-
-        woven = [[keep.tile([P, PIECE, 4], BF16, name=f"woven{z}_{i}", align_bytes=64) for i in range(PIECES)] for z in range(2)]
-        codes = [[keep.tile([P, PIECE], U32, name=f"codes{z}_{i}", align_bytes=64) for i in range(PIECES)] for z in range(2)]
-        scale = [[keep.tile([P, PIECE], U8, name=f"scale{z}_{i}", align_bytes=64) for i in range(PIECES)] for z in range(2)]
-        flat = {}
-
-        def gather(z, t, i):
-            window = planes[4 * z + t][:].indirect(entries(picked, i * PIECE, (i + 1) * PIECE))
-            if i == 0:
-                nc.vector.tensor_copy(woven[z][0][:, :, t], window)
+            dst = spread[i][:].rearrange("p (n c) -> p n c", c=4)
+            src = spread_ps[i][:].rearrange("p (c n) -> p n c", c=4)
+            if i % 2 == 0:
+                nc.vector.tensor_copy(dst, src)
             else:
-                if t % 2 == 0:
-                    flat[z, t // 2, i] = keep.tile([P, 2, PIECE], BF16, name=f"flat{z}_{t // 2}_{i}")
-                nc.scalar.activation(flat[z, t // 2, i][:, t % 2, :], window, COPY)
+                nc.scalar.activation(dst, src, COPY)
 
-        def place(z, u, i, on_scalar=False):
-            dst = woven[z][i][:, :, 2 * u : 2 * u + 2]
-            src = flat[z, u, i][:].rearrange("p u n -> p n u")
+        codes = [[keep.tile([P, HALF], U32, name=f"codes{z}_{h}", align_bytes=64) for h in range(2)] for z in range(2)]
+        scale = [[keep.tile([P, HALF], U8, name=f"scale{z}_{h}", align_bytes=64) for h in range(2)] for z in range(2)]
+        woven = {}
+        for z, parts in enumerate(PARTS):
+            for lo, hi in parts:
+                woven[z, lo] = keep.tile([P, hi - lo, 4], BF16, name=f"woven{z}_{lo}", align_bytes=64)
+
+        def place_of(z, lo, hi):
+            first = max(a for a, end in PARTS[z] if a <= lo)
+            return woven[z, first][:, lo - first : hi - first, :]
+
+        flat = {}
+        for z in range(2):
+            for u in range(2):
+                for lo, hi in FLATS[z][u]:
+                    flat[z, u, lo] = keep.tile([P, 2, hi - lo], BF16, name=f"flat{z}_{u}_{lo}")
+
+        def flat_of(z, u, lo, hi):
+            first = max(a for a, end in FLATS[z][u] if a <= lo)
+            return flat[z, u, first][:, :, lo - first : hi - first]
+
+        def window(z, t, lo, hi):
+            return planes[4 * z + t][:].indirect(entries(picked, lo, hi))
+
+        def direct(z, t):
+            nc.vector.tensor_copy(place_of(z, 0, PIECE)[:, :, t], window(z, t, 0, PIECE))
+
+        def by_vector(z, t, lo, hi):
+            nc.vector.tensor_copy(flat_of(z, t // 2, lo, hi)[:, t % 2, :], window(z, t, lo, hi))
+
+        def by_scalar(z, t, lo, hi):
+            nc.scalar.activation(flat_of(z, t // 2, lo, hi)[:, t % 2, :], window(z, t, lo, hi), COPY)
+
+        def place(z, u, lo, hi, on_scalar=False):
+            dst = place_of(z, lo, hi)[:, :, 2 * u : 2 * u + 2]
+            src = flat_of(z, u, lo, hi).rearrange("p u n -> p n u")
             if on_scalar:
                 nc.scalar.activation(dst, src, COPY)
             else:
                 nc.vector.tensor_copy(dst, src)
 
-        def quantise(z, i):
+        def quantise(z, lo, hi):
+            h, cols = lo // HALF, slice(lo % HALF, lo % HALF + hi - lo)
             nc.vector.quantize_mx(
-                out=codes[z][i][:].bitcast(FP8X4), scales=scale[z][i][:], in_=woven[z][i][:].rearrange("p n t -> p (n t)")
+                out=codes[z][h][:, cols].bitcast(FP8X4),
+                scales=scale[z][h][:, cols],
+                in_=place_of(z, lo, hi).rearrange("p n t -> p (n t)"),
             )
 
-        def product(bank, b, z, i):
+        def product(bank, b, z, lo, hi):
+            h, cols = lo // HALF, slice(lo % HALF, lo % HALF + hi - lo)
             nc.tensor.matmul_mx(
                 out=bank,
                 lhsT=w_words[z][:, b * P : (b + 1) * P].bitcast(FP8X4),
                 lhsT_scale=w_scale[4 * z : P, b * P : (b + 1) * P],
-                rhs=codes[z][i][:].bitcast(FP8X4),
-                rhs_scale=scale[z][i][:],
+                rhs=codes[z][h][:, cols].bitcast(FP8X4),
+                rhs_scale=scale[z][h][:, cols],
                 start=(z == 0),
                 stop=(z == 1),
             )
 
-        for z in range(2):
-            for t in range(4):
-                for i in range(PIECES):
-                    gather(z, t, i)
-                if z == 0:
-                    unload_weight(t)
-                if t % 2 == 1 and (z, t) != (1, 3):
-                    for i in range(1, PIECES):
-                        place(z, t // 2, i)
-            if z == 0:
-                for i in range(PIECES):
-                    quantise(0, i)
-        banks = [[psum.tile([P, 512], F32, name=f"y_ps{b}_{i}", tag=f"bank{4 * b + i}") for i in range(PIECES)] for b in range(2)]
-        for i in range(PIECES):
-            product(banks[0][i][:, 0:PIECE], 0, 0, i)
-        place(1, 1, 1)
-        quantise(1, 0)
-        place(1, 1, 2)
-        quantise(1, 1)
-        place(1, 1, 3, on_scalar=True)
-        quantise(1, 2)
-        quantise(1, 3)
+        for row in range(7):
+            z, t = divmod(row, 4)
+            cut = 2 * PIECE if row in (0, 1, 2, 6) else PIECE
+            direct(z, t)
+            if cut > PIECE:
+                by_vector(z, t, PIECE, cut)
+            for lo, hi in FLATS[z][t // 2]:
+                if hi > cut:
+                    by_scalar(z, t, max(lo, cut), hi)
+            if row < 2:
+                unload_weight(2 * row)
+                unload_weight(2 * row + 1)
+            if t % 2 == 1:
+                for lo, hi in PARTS[z]:
+                    if hi > PIECE:
+                        place(z, t // 2, max(lo, PIECE), hi)
+            if row == 3:
+                for lo, hi in PARTS[0]:
+                    quantise(0, lo, hi)
+        direct(1, 3)
+        for lo, hi in FLATS[1][1]:
+            by_scalar(1, 3, lo, hi)
+        parts = PARTS[1]
+        banks0 = [psum.tile([P, 512], F32, name=f"y0_ps{i}", tag=f"bank{i}") for i in range(len(parts))]
+        banks1 = [psum.tile([P, 512], F32, name=f"y1_ps{h}", tag=f"bank{5 + h}") for h in range(2)]
+        for bank, (lo, hi) in zip(banks0, parts):
+            product(bank[:, 0 : hi - lo], 0, 0, lo, hi)
+        place(1, 1, *parts[1])
+        quantise(1, *parts[0])
+        place(1, 1, *parts[2])
+        quantise(1, *parts[1])
+        place(1, 1, *parts[3])
+        place(1, 1, *parts[4], on_scalar=True)
+        for part in parts[2:]:
+            quantise(1, *part)
         y = [keep.tile([P, S], F32, name=f"y{b}") for b in range(2)]
-        for i in range(PIECES):
-            product(banks[0][i][:, 0:PIECE], 0, 1, i)
-            nc.scalar.activation(y[0][:, i * PIECE : (i + 1) * PIECE], banks[0][i][:, 0:PIECE], COPY)
-        for i in range(PIECES):
-            product(banks[1][i][:, 0:PIECE], 1, 0, i)
-            product(banks[1][i][:, 0:PIECE], 1, 1, i)
-        for i in range(2):
-            nc.vector.tensor_copy(y[1][:, i * PIECE : (i + 1) * PIECE], banks[1][i][:, 0:PIECE])
+        for bank, (lo, hi) in zip(banks0, parts):
+            product(bank[:, 0 : hi - lo], 0, 1, lo, hi)
+            if hi - lo == PIECE:
+                nc.scalar.activation(y[0][:, lo:hi], bank[:, 0 : hi - lo], COPY)
+            else:
+                nc.vector.tensor_copy(y[0][:, lo:hi], bank[:, 0 : hi - lo])
+        for h in range(2):
+            for z in range(2):
+                product(banks1[h][:], 1, z, h * HALF, (h + 1) * HALF)
+
+        got = [{i: keep.tile([P, V], F32, name=f"got{b}_{i}") for i in range(4) if (b, i) not in ((1, 1), (1, 3))} for b in range(2)]
+        plain = {key: keep.tile([P, V], F32, name=f"plain{key[0]}_{key[1]}") for key in ((0, 2), (0, 3), (1, 2))}
+        got[1][1] = plain[1, 2]
+        got[1][3] = plain[0, 3]
+        summed = [keep.tile([P, V], F32, name=f"summed{b}") for b in range(2)]
+        result = [keep.tile([P, V], F32, name=f"result{b}") for b in range(2)]
+        stretches = ((0, 0, V), (1, 0, V // 2), (1, V // 2, V))
+        turned = {key: psum.tile([P, V], F32, name=f"turned{i}", tag=f"bank{i}") for i, key in enumerate(stretches)}
+        acc = {key: psum.tile([P, V], F32, name=f"acc{i}", tag=f"bank{(3, 4, 7)[i]}") for i, key in enumerate(stretches)}
 
         def fused(b, i, lo=0, hi=V):
             nc.vector.tensor_tensor(got[b][i][:, lo:hi], y[b][:].indirect(entries(corner[i], lo, hi)), spread[i][:, lo:hi], MULT)
@@ -163,60 +215,58 @@ def tile_picked_bilin_none_e_kernel(
         def fetch(b, i):
             nc.scalar.activation(plain[b, i][:], y[b][:].indirect(corner[i][:]), COPY)
 
-        def weigh(b, i):
-            nc.vector.tensor_tensor(got[b][i][:], plain[b, i][:], spread[i][:], MULT)
+        def weigh(b, i, lo=0, hi=V):
+            nc.vector.tensor_tensor(got[b][i][:, lo:hi], plain[b, i][:, lo:hi], spread[i][:, lo:hi], MULT)
 
-        def turn(b, i, first, last):
-            for c in range(4):
+        def turn(key, i, first, last):
+            b, lo, hi = key
+            for c in range(lo, hi, P):
                 nc.tensor.matmul(
-                    turned[b][:, c * P : (c + 1) * P],
-                    got[b][i][:, c * P : (c + 1) * P],
+                    turned[key][:, c - lo : c - lo + P],
+                    got[b][i][:, c : c + P],
                     ident[:],
-                    start=(first and c == 0),
-                    stop=(last and c == 3),
+                    start=(first and c == lo),
+                    stop=(last and c == hi - P),
                     is_transpose=True,
                 )
 
-        def turn_back(b):
-            for h in range(2):
-                nc.scalar.activation(summed[b][:, h * 256 : (h + 1) * 256], turned[b][:, h * 256 : (h + 1) * 256], COPY)
-            for c in range(4):
-                nc.tensor.transpose(acc[b][:, c * P : (c + 1) * P], summed[b][:, c * P : (c + 1) * P], ident[:])
+        def turn_back(key):
+            b, lo, hi = key
+            nc.scalar.activation(summed[b][:, lo:hi], turned[key][:, 0 : hi - lo], COPY)
+            for c in range(lo, hi, P):
+                nc.tensor.transpose(acc[key][:, c - lo : c - lo + P], summed[b][:, c : c + P], ident[:])
 
-        got = [[keep.tile([P, V], F32, name=f"got{b}_{i}") for i in range(4)] for b in range(2)]
-        plain = {(b, i): keep.tile([P, V], F32, name=f"plain{b}_{i}") for b in range(2) for i in (2, 3)}
-        summed = [keep.tile([P, V], F32, name=f"summed{b}") for b in range(2)]
-        result = [keep.tile([P, V], F32, name=f"result{b}") for b in range(2)]
-        turned = [psum.tile([P, V], F32, name=f"turned{b}", tag=f"bank{b}") for b in range(2)]
-        acc = [psum.tile([P, V], F32, name=f"acc{b}", tag=f"bank{2 + b}") for b in range(2)]
-
+        whole, left, right = stretches
         fetch(0, 2)
+        for h in range(2):
+            nc.scalar.activation(y[1][:, h * HALF : (h + 1) * HALF], banks1[h][:], COPY)
         fetch(0, 3)
-        for i in range(2, PIECES):
-            nc.scalar.activation(y[1][:, i * PIECE : (i + 1) * PIECE], banks[1][i][:, 0:PIECE], COPY)
         fetch(1, 2)
-        fetch(1, 3)
         fused(0, 0)
-        turn(0, 0, True, False)
-        weigh(0, 2)
-        turn(0, 2, False, False)
+        turn(whole, 0, True, False)
         fused(0, 1)
-        turn(0, 1, False, False)
-        weigh(0, 3)
-        turn(0, 3, False, True)
+        turn(whole, 1, False, False)
+        weigh(0, 2)
+        turn(whole, 2, False, False)
         fused(1, 0)
-        turn(1, 0, True, False)
-        weigh(1, 2)
-        turn(1, 2, False, False)
-        weigh(1, 3)
-        turn(1, 3, False, True)
-        turn_back(0)
-        turn_back(1)
-        nc.scalar.activation(result[0][:], acc[0][:], COPY)
+        turn(left, 0, True, False)
+        turn(right, 0, True, False)
+        weigh(0, 3)
+        turn(whole, 3, False, True)
+        fused(1, 3)
+        turn(left, 3, False, False)
+        turn(right, 3, False, False)
+        for key in (left, right):
+            weigh(1, 2, key[1], key[2])
+            turn(key, 2, False, True)
+        turn_back(whole)
+        nc.scalar.activation(result[0][:], acc[whole][:], COPY)
         nc.sync.dma_start(out[0:P, :], result[0][:])
-        for lo in (0, V // 2):
-            fused(1, 1, lo, lo + V // 2)
-        for lo in (0, V // 2):
-            hi = lo + V // 2
-            nc.vector.tensor_tensor(result[1][:, lo:hi], got[1][1][:, lo:hi], acc[1][:, lo:hi], ADD)
+        turn_back(left)
+        turn_back(right)
+        for key in (left, right):
+            fused(1, 1, key[1], key[2])
+        for key in (left, right):
+            lo, hi = key[1], key[2]
+            nc.vector.tensor_tensor(result[1][:, lo:hi], got[1][1][:, lo:hi], acc[key][:, 0 : hi - lo], ADD)
             nc.sync.dma_start(out[P : 2 * P, lo:hi], result[1][:, lo:hi])

from contextlib import ExitStack

import concourse.mybir as mybir
from concourse.masks import make_identity

K, T, S, V, N = 1024, 2048, 1024, 512, 256
P = 128
FLOPS = 2 * K * N * S

F32 = mybir.dt.float32
BF16 = mybir.dt.bfloat16
U32 = mybir.dt.uint32
I32 = mybir.dt.int32
U16 = mybir.dt.uint16
U8 = mybir.dt.uint8
FP8X4 = mybir.dt.float8_e4m3fn_x4
COPY = mybir.ActivationFunctionType.Copy
MULT = mybir.AluOpType.mult
ADD = mybir.AluOpType.add

PIECE = 256
HALF = 512
PARTS = (((0, 512), (512, 1024)), ((0, 256), (256, 512), (512, 768), (768, 896), (896, 1024)))
FLATS = (
    (((256, 1024),), ((256, 1024),)),
    (((256, 1024),), ((256, 512), (512, 768), (768, 1024))),
)


def tile_picked_bilin_none_e_kernel(
    tc, xT, w1_words, w1_scales, fx, fy, offs, c00, c01, c10, c11, out
):
    nc = tc.nc
    with ExitStack() as ctx:
        keep = ctx.enter_context(tc.tile_pool(name="keep", bufs=1))
        psum = ctx.enter_context(tc.psum_pool(name="psum", bufs=1))

        def entries(lst, lo, hi):
            return lst[:, lo // 16 : hi // 16]

        ident = keep.tile([P, P], F32, name="ident")
        w_scale = keep.tile([P, N], U8, name="w_scale", align_bytes=64)
        nc.gpsimd.memset(w_scale[:].bitcast(I32), 0)
        make_identity(nc, ident[:])

        picked = keep.tile([P, S // 16], U16, name="picked")
        sides = keep.tile([P, 2, 2, 4], F32, name="sides")
        for axis, frac in enumerate((fx, fy)):
            nc.scalar.dma_start(sides[:, axis, 1, :], frac[0:1, :].rearrange("o (p c) -> (o p) c", c=4))
        planes = []
        for z in range(2):
            rows = xT[512 * z : 512 * (z + 1), :].rearrange("(p t) c -> p t c", t=4)
            for t in range(4):
                plane = keep.tile([P, T], F32, name=f"plane{z}_{t}")
                nc.sync.dma_start(plane[:], rows[:, t, :])
                planes.append(plane)
                if (z, t) == (0, 0):
                    nc.sync.dma_start(picked[:], offs)
        for q in range(4):
            nc.sync.dma_start(w_scale[32 * q : 32 * q + 8, :].bitcast(I32), w1_scales[:, 4 * q : 4 * q + 4, :].bitcast(I32))
        w_words = [keep.tile([P, N], U32, name=f"w_words{z}", align_bytes=64) for z in range(2)]
        for z in range(2):
            nc.sync.dma_start(w_words[z][:].bitcast(I32), w1_words[z].rearrange("p n t -> p (n t)").bitcast(I32))
        corner = []
        for i, lst in enumerate((c00, c01, c10, c11)):
            tile = keep.tile([P, V // 16], U16, name=f"corner{i}")
            nc.sync.dma_start(tile[:], lst)
            corner.append(tile)

        nc.gpsimd.tensor_scalar(sides[:, :, 0, :], sides[:, :, 1, :], -1.0, 1.0, MULT, ADD)
        weight = keep.tile([P, 16], F32, name="weight")
        nc.gpsimd.tensor_tensor(
            weight[:].rearrange("p (j i c) -> p j i c", j=2, i=2),
            sides[:, 0, :, :].unsqueeze(1).to_broadcast([P, 2, 2, 4]),
            sides[:, 1, :, :].unsqueeze(2).to_broadcast([P, 2, 2, 4]),
            MULT,
        )
        spread_ps = []
        for i in range(4):
            bank = psum.tile([P, V], F32, name=f"spread_ps{i}", tag=f"bank{4 + i}")
            spread_ps.append(bank)
            for c in range(4):
                column = weight[:, 4 * i + c : 4 * i + c + 1]
                nc.tensor.transpose(bank[:, c * P : (c + 1) * P], column.to_broadcast([P, P]), ident[:])
        spread = [keep.tile([P, V], F32, name=f"spread{i}") for i in range(4)]

        def unload_weight(i):
            dst = spread[i][:].rearrange("p (n c) -> p n c", c=4)
            src = spread_ps[i][:].rearrange("p (c n) -> p n c", c=4)
            if i % 2 == 0:
                nc.vector.tensor_copy(dst, src)
            else:
                nc.scalar.activation(dst, src, COPY)

        codes = [[keep.tile([P, HALF], U32, name=f"codes{z}_{h}", align_bytes=64) for h in range(2)] for z in range(2)]
        scale = [[keep.tile([P, HALF], U8, name=f"scale{z}_{h}", align_bytes=64) for h in range(2)] for z in range(2)]
        woven = {}
        for z, parts in enumerate(PARTS):
            for lo, hi in parts:
                woven[z, lo] = keep.tile([P, hi - lo, 4], BF16, name=f"woven{z}_{lo}", align_bytes=64)

        def place_of(z, lo, hi):
            first = max(a for a, end in PARTS[z] if a <= lo)
            return woven[z, first][:, lo - first : hi - first, :]

        flat = {}
        for z in range(2):
            for u in range(2):
                for lo, hi in FLATS[z][u]:
                    flat[z, u, lo] = keep.tile([P, 2, hi - lo], BF16, name=f"flat{z}_{u}_{lo}")

        def flat_of(z, u, lo, hi):
            first = max(a for a, end in FLATS[z][u] if a <= lo)
            return flat[z, u, first][:, :, lo - first : hi - first]

        def window(z, t, lo, hi):
            return planes[4 * z + t][:].indirect(entries(picked, lo, hi))

        def direct(z, t):
            nc.vector.tensor_copy(place_of(z, 0, PIECE)[:, :, t], window(z, t, 0, PIECE))

        def by_vector(z, t, lo, hi):
            nc.vector.tensor_copy(flat_of(z, t // 2, lo, hi)[:, t % 2, :], window(z, t, lo, hi))

        def by_scalar(z, t, lo, hi):
            nc.scalar.activation(flat_of(z, t // 2, lo, hi)[:, t % 2, :], window(z, t, lo, hi), COPY)

        def place(z, u, lo, hi, on_scalar=False):
            dst = place_of(z, lo, hi)[:, :, 2 * u : 2 * u + 2]
            src = flat_of(z, u, lo, hi).rearrange("p u n -> p n u")
            if on_scalar:
                nc.scalar.activation(dst, src, COPY)
            else:
                nc.vector.tensor_copy(dst, src)

        def quantise(z, lo, hi):
            h, cols = lo // HALF, slice(lo % HALF, lo % HALF + hi - lo)
            nc.vector.quantize_mx(
                out=codes[z][h][:, cols].bitcast(FP8X4),
                scales=scale[z][h][:, cols],
                in_=place_of(z, lo, hi).rearrange("p n t -> p (n t)"),
            )

        def product(bank, b, z, lo, hi):
            h, cols = lo // HALF, slice(lo % HALF, lo % HALF + hi - lo)
            nc.tensor.matmul_mx(
                out=bank,
                lhsT=w_words[z][:, b * P : (b + 1) * P].bitcast(FP8X4),
                lhsT_scale=w_scale[4 * z : P, b * P : (b + 1) * P],
                rhs=codes[z][h][:, cols].bitcast(FP8X4),
                rhs_scale=scale[z][h][:, cols],
                start=(z == 0),
                stop=(z == 1),
            )

        for row in range(7):
            z, t = divmod(row, 4)
            cut = 2 * PIECE if row in (0, 1, 2, 6) else PIECE
            direct(z, t)
            if cut > PIECE:
                by_vector(z, t, PIECE, cut)
            for lo, hi in FLATS[z][t // 2]:
                if hi > cut:
                    by_scalar(z, t, max(lo, cut), hi)
            if row < 2:
                unload_weight(2 * row)
                unload_weight(2 * row + 1)
            if t % 2 == 1:
                for lo, hi in PARTS[z]:
                    if hi > PIECE:
                        place(z, t // 2, max(lo, PIECE), hi)
            if row == 3:
                for lo, hi in PARTS[0]:
                    quantise(0, lo, hi)
        direct(1, 3)
        for lo, hi in FLATS[1][1]:
            by_scalar(1, 3, lo, hi)
        parts = PARTS[1]
        banks0 = [psum.tile([P, 512], F32, name=f"y0_ps{i}", tag=f"bank{i}") for i in range(len(parts))]
        banks1 = [psum.tile([P, 512], F32, name=f"y1_ps{h}", tag=f"bank{5 + h}") for h in range(2)]
        for bank, (lo, hi) in zip(banks0, parts):
            product(bank[:, 0 : hi - lo], 0, 0, lo, hi)
        place(1, 1, *parts[1])
        quantise(1, *parts[0])
        place(1, 1, *parts[2])
        quantise(1, *parts[1])
        place(1, 1, *parts[3])
        place(1, 1, *parts[4], on_scalar=True)
        for part in parts[2:]:
            quantise(1, *part)
        y = [keep.tile([P, S], F32, name=f"y{b}") for b in range(2)]
        for bank, (lo, hi) in zip(banks0, parts):
            product(bank[:, 0 : hi - lo], 0, 1, lo, hi)
            if hi - lo == PIECE:
                nc.scalar.activation(y[0][:, lo:hi], bank[:, 0 : hi - lo], COPY)
            else:
                nc.vector.tensor_copy(y[0][:, lo:hi], bank[:, 0 : hi - lo])
        for h in range(2):
            for z in range(2):
                product(banks1[h][:], 1, z, h * HALF, (h + 1) * HALF)

        got = [{i: keep.tile([P, V], F32, name=f"got{b}_{i}") for i in range(4) if (b, i) not in ((1, 1), (1, 3))} for b in range(2)]
        plain = {key: keep.tile([P, V], F32, name=f"plain{key[0]}_{key[1]}") for key in ((0, 2), (0, 3), (1, 2))}
        got[1][1] = plain[1, 2]
        got[1][3] = plain[0, 3]
        summed = [keep.tile([P, V], F32, name=f"summed{b}") for b in range(2)]
        result = [keep.tile([P, V], F32, name=f"result{b}") for b in range(2)]
        stretches = ((0, 0, V), (1, 0, V // 2), (1, V // 2, V))
        turned = {key: psum.tile([P, V], F32, name=f"turned{i}", tag=f"bank{i}") for i, key in enumerate(stretches)}
        acc = {key: psum.tile([P, V], F32, name=f"acc{i}", tag=f"bank{(3, 4, 7)[i]}") for i, key in enumerate(stretches)}

        def fused(b, i, lo=0, hi=V):
            nc.vector.tensor_tensor(got[b][i][:, lo:hi], y[b][:].indirect(entries(corner[i], lo, hi)), spread[i][:, lo:hi], MULT)

        def fetch(b, i):
            nc.scalar.activation(plain[b, i][:], y[b][:].indirect(corner[i][:]), COPY)

        def weigh(b, i, lo=0, hi=V):
            nc.vector.tensor_tensor(got[b][i][:, lo:hi], plain[b, i][:, lo:hi], spread[i][:, lo:hi], MULT)

        def turn(key, i, first, last):
            b, lo, hi = key
            for c in range(lo, hi, P):
                nc.tensor.matmul(
                    turned[key][:, c - lo : c - lo + P],
                    got[b][i][:, c : c + P],
                    ident[:],
                    start=(first and c == lo),
                    stop=(last and c == hi - P),
                    is_transpose=True,
                )

        def turn_back(key):
            b, lo, hi = key
            nc.scalar.activation(summed[b][:, lo:hi], turned[key][:, 0 : hi - lo], COPY)
            for c in range(lo, hi, P):
                nc.tensor.transpose(acc[key][:, c - lo : c - lo + P], summed[b][:, c : c + P], ident[:])

        whole, left, right = stretches
        fetch(0, 2)
        for h in range(2):
            nc.scalar.activation(y[1][:, h * HALF : (h + 1) * HALF], banks1[h][:], COPY)
        fetch(0, 3)
        fetch(1, 2)
        fused(0, 0)
        turn(whole, 0, True, False)
        fused(0, 1)
        turn(whole, 1, False, False)
        weigh(0, 2)
        turn(whole, 2, False, False)
        fused(1, 0)
        turn(left, 0, True, False)
        turn(right, 0, True, False)
        weigh(0, 3)
        turn(whole, 3, False, True)
        fused(1, 3)
        turn(left, 3, False, False)
        turn(right, 3, False, False)
        for key in (left, right):
            weigh(1, 2, key[1], key[2])
            turn(key, 2, False, True)
        turn_back(whole)
        nc.scalar.activation(result[0][:], acc[whole][:], COPY)
        nc.sync.dma_start(out[0:P, :], result[0][:])
        turn_back(left)
        turn_back(right)
        for key in (left, right):
            fused(1, 1, key[1], key[2])
        for key in (left, right):
            lo, hi = key[1], key[2]
            nc.vector.tensor_tensor(result[1][:, lo:hi], got[1][1][:, lo:hi], acc[key][:, 0 : hi - lo], ADD)
            nc.sync.dma_start(out[P : 2 * P, lo:hi], result[1][:, lo:hi])
